import numpy as np, ml_dtypes
CORES = [25,29,65,69,153,157,193,197]
N = 8
BF = ml_dtypes.bfloat16
S, U, NP, CAP, FO, RO = 2560, 2048, 192, 32, 2, 4
G = NP + FO * CAP
def parts(rng):
    x = rng.integers(0, 256, (N, 8, 16, S)); kd = rng.integers(0, 4096, (N, 16, U)); wt = rng.integers(0, 256, (N, 8, 16, 1))
    th = rng.integers(64, 208, (N, 8, 16, 1)); th = np.where(rng.random(th.shape) < 0.06, 256 * rng.integers(0, 2, th.shape), th)
    tau = rng.integers(900, 1700, (N, 8, 1, 1)) + rng.integers(-150, 151, (N, 8, 16, 1))
    return x, kd, wt, th, tau
def pack(x, kd, wt, th, tau):
    col = lambda a: np.ascontiguousarray(a.reshape(N, 128, 1)).astype(np.int32)
    return {"x0": np.ascontiguousarray(x.reshape(N, 128, S)).astype(np.float32).astype(BF), "kd": kd.astype(np.int32), "wt": col(wt), "th": col(th), "tau": col(tau)}
def draw_of(a):
    return (a * 4096 + S - 1) // S
def apart(rng, n):
    got = []; used = {0}
    for d in rng.permutation(np.arange(64, 4096 * S // (S + (RO - 1) * G))):
        v = {int(d) * (S + t * G) >> 12 for t in range(RO)}
        if len(v) == RO and not v & used:
            got.append(int(d)); used |= v
        if len(got) == n: break
    return np.array(got)
def columns_of(rng, h):
    z = h[:, None, :] // 16 + (np.arange(16)[None, :, None] < h[:, None, :] % 16)
    a, b = z[:, ::2], z[:, 1::2]; s = rng.integers(0, np.minimum(a, 255 - b) + 1); z = np.concatenate([a - s, b + s], axis=1)
    return np.take_along_axis(z, np.argsort(rng.random(z.shape), axis=1), 1)
def setup_inputs(rng):
    return pack(*parts(rng))
def setup_inputs_corners(rng):
    x, kd, wt, th, tau = parts(rng)
    kd = np.where(rng.random(kd.shape) < 0.3, 4095 * rng.integers(0, 2, kd.shape), kd); ui = (613 * np.arange(NP)) & (U - 1)
    for a in range(N):
        o = 2 + rng.permutation(S - 2); o = np.concatenate([[0], o[:NP - 1], [1], o[NP - 1:]]); p, q = o[:NP], o[NP:2 * NP]
        first = rng.random((16, NP)) < 0.5; first[0] = True; first[15] = False
        kd[a][:, ui] = draw_of(np.where(first, p[None, :], q[None, :]))
        cnt = rng.permutation(np.array([0, 1, CAP - 1, CAP, CAP + 1, NP]))
        for g in range(6):
            m = rng.permutation(NP)[:int(cnt[g])]
            wt[a, g] = 0; th[a, g] = 256 * rng.integers(0, 2, (16, 1)); th[a, g, 0] = 0
            tau[a, g] = rng.choice(np.array([0, 1, 1000, 1500, 4079, 4080]), (16, 1)); tau[a, g, 0] = 4079
            x[a, g][:, q] = x[a, g][:, p]; x[a, g][:, p[m]] = 0; x[a, g][:, q[m]] = 255
        wt[a, 6] = 255; th[a, 6] = rng.choice(np.array([0, 1, 128, 255, 256]), (16, 1)); tau[a, 6] = rng.choice(np.array([0, 1300, 4080]), (16, 1))
        th[a, 7] = 256
    return pack(x, kd, wt, th, tau)
def setup_inputs_deep(rng):
    x, kd, wt, th, tau = parts(rng)
    near = 4095 - np.floor(300 * rng.random(kd.shape) ** 2).astype(np.int64)
    kd = np.where(rng.random(kd.shape) < 0.7, near, kd); th = rng.integers(90, 140, th.shape)
    tau = np.minimum(rng.choice(np.array([0, 300, 600, 900, 1200, 4080]), (N, 8, 1, 1)) + rng.integers(0, 200, (N, 8, 16, 1)), 4080)
    tau[:, 2] = 4080; tau[:, 5] = 0
    return pack(x, kd, wt, th, tau)
def setup_inputs_ends(rng):
    x = 255 * rng.integers(0, 2, (N, 8, 16, S)); x = np.where(rng.random((N, 8, 1, S)) < 0.4, 255 * rng.integers(0, 2, (N, 8, 1, S)), x)
    wt = 255 * rng.integers(0, 2, (N, 8, 16, 1)); sh = wt.shape
    th = np.where(rng.random(sh) < 0.75, 256 * rng.integers(0, 2, sh), rng.choice(np.array([1, 128, 255]), sh))
    tau = np.where(rng.random(sh) < 0.7, 4080 * rng.integers(0, 2, sh), 255 * rng.integers(0, 17, sh))
    end = (rng.random((N, 1, U)) < 0.5) | (rng.random((N, 16, U)) < 0.5)
    kd = np.where(end, 4095 * rng.integers(0, 2, (N, 16, U)), rng.integers(0, 4096, (N, 16, U)))
    bits = rng.integers(0, 2, (N, 1, S)); bits[..., 0] = 0; bits[..., S - 1] = 1; bits[..., S - G] = 1; bits[..., S - G + 1] = 0; bits[..., S - G + NP - 1] = 1
    x[:, 7] = 255 * bits; wt[:, 7] = 255
    th[:, 7] = 256 * rng.integers(0, 2, (N, 16, 1)); th[:, 7, 0] = 0; th[:, 7, 1] = 256; th[:, 7, 14] = 0; th[:, 7, 15] = 0
    tau[:, 7] = 4080 * rng.integers(0, 2, (N, 16, 1)); tau[:, 7, 0] = 4080; tau[:, 7, 14] = 4080; tau[:, 7, 15] = 0
    i = 613 * np.arange(NP); both = np.unique(np.concatenate([i & (U - 1), (i + 16 * 255 * 255) & (U - 1)]))
    kd[:, :, both] = 4095 * rng.integers(0, 2, (N, 16, len(both))); kd[:, 1, both] = 4095; kd[:, 15, both] = 0; kd[:, 0, 0] = 0
    e = np.array([613 * (CAP - 1), 613 * (NP - 1)]); e = np.concatenate([e, e + 16 * 255 * 255]) & (U - 1)
    kd[:, :, e] = 4095; kd[:, 15, e] = 0; kd[:, 0, (e + 1) & (U - 1)] = 4095
    return pack(x, kd, wt, th, tau)
def setup_inputs_spread(rng):
    x, kd, wt, th, tau = parts(rng); sh = wt.shape
    x = np.minimum(np.floor(np.exp2(8 * rng.random((N, 8, 1, S))) * rng.random((N, 8, 16, S))), 255).astype(np.int64)
    kd = np.minimum(np.floor(4096 * rng.random((N, 16, U)) ** np.exp2(rng.integers(-2, 3, (N, 1, U)))), 4095).astype(np.int64)
    wt = np.minimum(np.floor(np.exp2(8 * rng.random(sh))) - 1, 255).astype(np.int64); wt[:, :, 3] = 255
    th = np.where(rng.random(sh) < 0.7, np.minimum(np.floor(np.exp2(8.01 * rng.random(sh))) - 1, 256), rng.integers(0, 257, sh)).astype(np.int64)
    tau = np.where(rng.random(sh) < 0.5, np.minimum(np.floor(np.exp2(12 * rng.random(sh))) - 1, 4080), rng.integers(200, 2200, sh)).astype(np.int64)
    return pack(x, kd, wt, th, tau)
def setup_inputs_turns(rng):
    x, kd, wt, th, tau = parts(rng); wt[...] = 0; ui = (613 * np.arange(NP)) & (U - 1); n = 20; tight = np.arange(n) % 2 == 0
    own = np.concatenate([np.arange(4), np.full(CAP - 2, 4), 5 + np.arange(NP - CAP - 2) % (n - 5)])
    pat = np.zeros((6, n), bool); pat[1, 0] = True; pat[2, [0, 4]] = True; pat[3, [0, 1, 4]] = True; pat[4, [0, 1, 2, 4]] = True; pat[5] = True
    q = rng.permutation(N)
    for a in range(N):
        d = apart(rng, n); c = rng.permutation(own); size = np.bincount(c, minlength=n)
        first = rng.random((16, NP)) < 0.5; first[0] = True; first[15] = False
        kd[a][:, ui] = np.where(first, d[c][None, :], 0)
        opt = rng.integers(0, 7, (RO, 8))
        if a == q[0]:
            opt[0] = rng.permutation(np.array([0, 1, 1, 1, 2, 3, 4, 5])); opt[1] = 0; opt[2] = rng.integers(1, 6, 8)
        if a == q[1]:
            opt[1] = 5; opt[2] = rng.integers(1, 6, 8)
        go = np.where((opt == 6)[..., None], rng.random((RO, 8, n)) < 0.5, pat[np.minimum(opt, 5)])
        least = rng.permutation(np.concatenate([np.array([0, 64, 2047, 2048, 4064]), rng.integers(100, 4065, 3)])); row = rng.integers(0, 16, 8)
        th[a, :, :, 0] = rng.choice(np.array([0, 0, 1, 128, 255, 256]), (8, 16))
        tau[a, :, :, 0] = np.minimum(least[:, None] + rng.choice(np.array([0, 0, 1, 15, 500, 4080]), (8, 16)), 4080)
        th[a, np.arange(8), row, 0] = 0; tau[a, np.arange(8), row, 0] = least
        count = 0
        for t in range(RO):
            lim = (least + (count & 15))[:, None]; v = (d * (S + t * G)) >> 12
            over = np.where(tight, 1, 1 + np.floor((4080 - lim) * rng.random((8, n))).astype(np.int64))
            under = np.where(tight, 0, np.floor((lim + 1) * rng.random((8, n))).astype(np.int64))
            x[a][:, :, v] = columns_of(rng, np.where(go[t], lim + over, lim - under))
            count = int(np.sum(size * go[t]))
        x[a][:, :, 0] = 0
    return pack(x, kd, wt, th, tau)
def check_inputs(d):
    bad = []
    for k, lo, hi in (("x0", 0, 255), ("kd", 0, 4095), ("wt", 0, 255), ("th", 0, 256), ("tau", 0, 4080)):
        a = np.asarray(d[k]).astype(np.float64)
        if not (np.all(a >= lo) and np.all(a <= hi) and np.all(a == np.floor(a))): bad.append("range of " + k)
    return bad
def reference(x0, kd, wt, th, tau):
    tot = S + RO * G
    X = np.zeros((N, 8, 16, tot), np.int64); X[..., :S] = x0.astype(np.float32).astype(np.int64).reshape(N, 8, 16, S)
    A = np.zeros((N, 8, 16, tot), np.int64); A[...] = np.arange(tot)
    tb = kd.astype(np.int64); w = wt.astype(np.int64).reshape(N, 8, 16, 1); lim = tau.astype(np.int64).reshape(N, 8, 16, 1); thr = th.astype(np.int64).reshape(N, 8, 16, 1, 1)
    C = [0] * N
    for t in range(RO):
        B = S + t * G
        u = (np.sum(w * X[..., B - G:B - G + NP], axis=2) + 613 * np.arange(NP)) & (U - 1)
        mail = []
        for a in range(N):
            e = (tb[a][:, u[a]] * B) >> 12
            ix = np.ascontiguousarray(e.transpose(1, 2, 0)).reshape(8, 1, NP * 16)
            xe = np.take_along_axis(X[a], ix, 2).reshape(8, 16, NP, 16); ne = np.take_along_axis(A[a], ix, 2).reshape(8, 16, NP, 16)
            m = xe >= thr[a]
            lo = np.min(np.where(m, ne, tot), axis=3); hi = np.max(np.where(m, ne, -1), axis=3); none = hi < 0
            lo = np.where(none, ne[..., 0], lo); hi = np.where(none, ne[..., 0], hi)
            xl = np.take_along_axis(X[a], lo.reshape(8, 1, 16 * NP), 2).reshape(8, 16, 16, NP)
            xh = np.take_along_axis(X[a], hi.reshape(8, 1, 16 * NP), 2).reshape(8, 16, 16, NP)
            D = np.sum(np.abs(xl - xh), axis=1)
            far = D > lim[a] + (C[a] & 15)
            A[a, :, :, B:B + NP] = np.where(far, np.arange(B, B + NP), lo)
            nx = (np.max(xl, axis=2) + np.min(xh, axis=2)) >> 1
            X[a, :, :, B:B + NP] = nx
            c = np.any(far, axis=1)
            C[a] = int(np.sum(c))
            o = np.argsort(np.where(c, 0, 1), axis=1, kind="stable")[:, :CAP]
            mail.append(np.where(np.take_along_axis(c, o, 1)[:, None, :], np.take_along_axis(nx, o[:, None, :], 2), 0))
        for a in range(N):
            for f in range(FO):
                q = (a - 1 - (FO * t + f) % (N - 1)) % N; b = B + NP + f * CAP
                X[a, :, :, b:b + CAP] = mail[q]
    return {"ya": A[..., S:].reshape(N, 128, RO * G).astype(np.float32), "yx": X[..., S:].reshape(N, 128, RO * G).astype(np.float32).astype(BF)}

@@ -1,0 +1,591 @@
+from concourse.bass import DstId, RemoteDMATransfer
+from concourse.mybir import AluOpType as Op, ActivationFunctionType as Fn
+
+S, U, NP, CAP, FO, RO = 2560, 2048, 192, 32, 2, 4
+G = NP + FO * CAP
+TOT = S + RO * G
+UP = 4096
+CHUNKS = [64, 64, 64]
+ORDER = "l0 l1 H0 a0 l2 h1 x0 e0 Y0 a1 d0 h2 b0 x1 e1 y1 n0 d1 a2 D0 Y2 b1 D1 x2 e2 n2 d2 f1 b2 f0 k0 k1 D2 n1 c0 c1 f2 k2 c2"
+
+SCRATCH = {
+    "X2": ("sbuf", [128, UP + TOT], "bfloat16"),
+    "Wl": ("sbuf", [128, 2 * TOT], "float32"),
+    "Wh": ("sbuf", [128, TOT], "float32"),
+    "kdt": ("sbuf", [128, U], "int32"),
+    "iof": ("sbuf", [128, TOT], "float32"),
+    "io16": ("sbuf", [128, S], "float16"),
+    "c14": ("sbuf", [128, 512], "bfloat16"),
+    "s8": ("sbuf", [128, S], "bfloat16"),
+    "s4": ("sbuf", [128, S], "bfloat16"),
+    "An": ("sbuf", [128, RO * G], "float32"),
+    "ci": ("sbuf", [128, 16], "int32"),
+    "cf": ("sbuf", [128, 16], "float32"),
+    "k613": ("sbuf", [128, 12], "float32"),
+    "wtc": ("sbuf", [128, 1], "int32"),
+    "thc": ("sbuf", [128, 1], "int32"),
+    "tac": ("sbuf", [128, 1], "int32"),
+    "wtf": ("sbuf", [128, 1], "float32"),
+    "thf": ("sbuf", [128, 1], "float32"),
+    "thr": ("sbuf", [128, 1], "float32"),
+    "cci": ("sbuf", [128, 2], "int32"),
+    "ones": ("sbuf", [128, 128], "bfloat16"),
+    "blk": ("sbuf", [128, 128], "bfloat16"),
+    "blk2": ("sbuf", [128, 128], "bfloat16"),
+    "idp": ("sbuf", [128, 128], "bfloat16"),
+    "idn": ("sbuf", [128, 128], "bfloat16"),
+    "idh": ("sbuf", [128, 128], "bfloat16"),
+    "ida": ("sbuf", [128, 128], "bfloat16"),
+    "idb": ("sbuf", [128, 128], "bfloat16"),
+    "on16": ("sbuf", [128, 128], "bfloat16"),
+    "id16": ("sbuf", [128, 128], "float16"),
+    "pm": ("sbuf", [128, 512], "float16"),
+    "om": ("sbuf", [128, 2048], "bfloat16"),
+    "wm": ("sbuf", [128, 2048], "bfloat16"),
+    "m8x": ("sbuf", [128, 512], "bfloat16"),
+    "m8n": ("sbuf", [128, 512], "bfloat16"),
+    "m16x": ("sbuf", [128, 1024], "bfloat16"),
+    "m16n": ("sbuf", [128, 1024], "bfloat16"),
+    "onesr": ("sbuf", [128, NP], "bfloat16"),
+    "ui": ("sbuf", [128, 12], "int32"),
+    "um": ("sbuf", [128, 12], "int32"),
+    "uo": ("sbuf", [128, 12], "uint16"),
+    "ke": ("sbuf", [128, NP], "float16"),
+    "tl1": ("sbuf", [128, 96], "uint16"),
+    "th1": ("sbuf", [128, 96], "uint16"),
+    "t2": ("sbuf", [128, 96], "uint16"),
+    "L1": ("sbuf", [128, 1536], "float32"),
+    "H1": ("sbuf", [128, 1536], "float32"),
+    "al": ("sbuf", [128, 1536], "float32"),
+    "ah": ("sbuf", [128, 1536], "float32"),
+    "sl": ("sbuf", [128, 1536], "float32"),
+    "sh": ("sbuf", [128, 1536], "float32"),
+    "hc": ("sbuf", [128, NP], "float32"),
+    "ol": ("sbuf", [128, NP], "uint16"),
+    "oh": ("sbuf", [128, NP], "uint16"),
+    "XL": ("sbuf", [128, 3072], "bfloat16"),
+    "XH": ("sbuf", [128, 3072], "bfloat16"),
+    "ad": ("sbuf", [128, 3072], "bfloat16"),
+    "mxs": ("sbuf", [128, 3072], "bfloat16"),
+    "mns": ("sbuf", [128, 3072], "bfloat16"),
+    "sm": ("sbuf", [128, NP], "float32"),
+    "si": ("sbuf", [128, NP], "int32"),
+    "nxb": ("sbuf", [128, 208], "bfloat16"),
+    "far": ("sbuf", [128, NP], "bfloat16"),
+    "flg": ("sbuf", [128, NP], "bfloat16"),
+    "cum": ("sbuf", [128, NP], "bfloat16"),
+    "sg": ("sbuf", [128, 2 * NP], "bfloat16"),
+    "cnt2": ("sbuf", [128, 2], "float32"),
+    "mo": ("sbuf", [128, 2], "uint16"),
+    "mailb": ("sbuf", [128, RO * CAP], "bfloat16"),
+    "rbuf": ("sbuf", [128, RO * CAP], "bfloat16"),
+    "lq": ("sbuf", [128, NP], "float32"),
+    "lt": ("sbuf", [128, NP], "float32"),
+    "fi": ("sbuf", [128, NP], "float32"),
+    "a4": ("sbuf", [128, NP], "float32"),
+    "e8": ("sbuf", [128, G], "bfloat16"),
+    "e4": ("sbuf", [128, G], "bfloat16"),
+    "iof4": ("sbuf", [128, RO * G], "float32"),
+    "q0": ("psum", [128, 512], "float32"),
+    "q1": ("psum", [128, 512], "float32"),
+    "q2": ("psum", [128, 512], "float32"),
+    "q3": ("psum", [128, 512], "float32"),
+    "pD": ("psum", [128, 512], "float32"),
+    "pX": ("psum", [128, 512], "float32"),
+    "pC": ("psum", [128, 512], "float32"),
+    "pU": ("psum", [128, 512], "float32"),
+}
+PSUM = ("q0", "q1", "q2", "q3", "pD", "pX", "pC", "pU")
+NDMA = 40
+SEMAPHORES = (["sv", "ss", "sp", "sg", "loc"] + ["ar%d" % t for t in range(RO)] + ["rl%d" % t for t in range(RO)]
+              + ["d%d" % i for i in range(NDMA)])
+
+
+def routes(T, topo):
+    n = len(T.cores)
+    relay = {}
+    plan = {}
+    for r in range(n):
+        src = T.cores[r]
+        far = [d for d in T.cores if d != src and not topo.may_write(src, d)]
+        relay[r] = [c for c in topo.cores_of(src) if c not in T.cores and topo.die(c) == topo.die(src)
+                    and all(topo.may_write(c, d) for d in far)][:2]
+        for t in range(RO):
+            ds = [T.cores[(r + 1 + ((FO * t + f) % (n - 1))) % n] for f in range(FO)]
+            plan[r, t] = ([(f, d) for f, d in enumerate(ds) if topo.may_write(src, d)],
+                          [(f, d) for f, d in enumerate(ds) if not topo.may_write(src, d)])
+    return relay, plan
+
+
+def emask(topo, src, dst, high, full=False):
+    es = topo.engines(src, dst)
+    if not full:
+        es = es[8:16] if high else es[:8]
+    return sum(1 << e for e in es), len(es)
+
+
+def land(t, f):
+    b = UP + S + t * G + NP + f * CAP
+    return b, b + CAP
+
+
+def relay_program(g, core, T, topo, r, which, plan):
+    sent = 0
+    for t in range(RO):
+        ds = plan[r, t][1][which:which + 1]
+        if not ds:
+            continue
+        n = emask(topo, T.cores[r], core, True, not plan[r, t][0])[1]
+        g.wait_ge(T.sem["rl%d" % t], n)
+        m, k = emask(topo, core, ds[0][1], False)
+        ids, outs = [], []
+        for f, d in ds:
+            rid, pid = topo.addr(d, core)
+            ids.append(DstId(rid=rid, pnc=pid))
+            a, b = land(t, f)
+            outs.append(T.X2[:, a:b])
+        g.remote_dma_fused([RemoteDMATransfer(dst_ids=ids, dma_engine_mask=m, remote_sem=T.sem["ar%d" % t],
+                                              srcs=[T.rbuf[:, t * CAP:(t + 1) * CAP]], dsts=outs)], local_sem=T.sem.loc)
+        sent += k
+    if sent:
+        g.wait_ge(T.sem.loc, sent)
+
+
+def rank_program(g, core, T, topo):
+    relay, plan = routes(T, topo)
+    rank = T.rank_of(core)
+    if rank is None:
+        for r in relay:
+            if core in relay[r]:
+                relay_program(g, core, T, topo, r, relay[r].index(core), plan)
+        return
+
+    queue = {"v": g.vector, "s": g.scalar, "p": g.tensor, "g": g, "y": g.sync}
+    semof = {"v": T.sem.sv, "s": T.sem.ss, "p": T.sem.sp, "g": T.sem.sg}
+    count = {"v": 0, "s": 0, "p": 0, "g": 0}
+    known = {q: {} for q in queue}
+    clock = {}
+    hist = {}
+    ndma = [0]
+
+    def need(q, reads, writes):
+        want = {}
+        for kind, regs in (("r", reads), ("w", writes)):
+            for name, a, b in regs:
+                ps = name in PSUM
+                for (hk, ha, hb, hq, hi) in hist.get(name, ()):
+                    if ps:
+                        if hq == q and hk == "r":
+                            continue
+                        if hq == q and (hb <= a or b <= ha):
+                            continue
+                    else:
+                        if hb <= a or b <= ha or (hk == "r" and kind == "r"):
+                            continue
+                        if hq == q and hk == "r":
+                            continue
+                    if want.get(hq, 0) < hi:
+                        want[hq] = hi
+        return want
+
+    def dowait(q, want):
+        for hq in sorted(want, key=lambda k: (k == q, k)):
+            hi = want[hq]
+            if known[q].get(hq, 0) >= hi:
+                continue
+            queue[q].wait_ge(semof[hq], hi)
+            for k2, v2 in clock[hq, hi].items():
+                if known[q].get(k2, 0) < v2:
+                    known[q][k2] = v2
+            known[q][hq] = hi
+
+    def note(q, hi, reads, writes):
+        for kind, regs in (("r", reads), ("w", writes)):
+            for name, a, b in regs:
+                hist.setdefault(name, []).append((kind, a, b, q, hi))
+
+    def op(q, fns, reads, writes, goes_on=False):
+        dowait(q, need(q, reads, [] if goes_on else writes))
+        for fn in fns:
+            fn().then_inc(semof[q], 1)
+            count[q] += 1
+            clock[q, count[q]] = dict(known[q])
+        note(q, count[q], reads, writes)
+
+    def dma(q, out, in_, reads, writes, alone=False):
+        if not alone:
+            dowait(q, need(q, reads, writes))
+        key = "d%d" % ndma[0]
+        ndma[0] += 1
+        semof[key] = T.sem[key]
+        queue[q].dma_start(out, in_).then_inc(T.sem[key], 16)
+        clock[key, 16] = dict(known[q])
+        note(key, 16, reads, writes)
+
+    def R(name, a, b, step=1):
+        return (T[name][:, a:b:step] if step != 1 else T[name][:, a:b], [(name, a, b)])
+
+    def I(win, a, b, off, c, d):
+        return (T[win][:, a:b].indirect(T[off][:, c:d]), [(win, a, b), (off, c, d)])
+
+    def col(name, j):
+        return R(name, j, j + 1)
+
+    def cp(q, out, in_):
+        if q == "v":
+            op("v", [lambda: g.vector.tensor_copy(out[0], in_[0])], in_[1], out[1])
+        else:
+            op("s", [lambda: g.scalar.activation(out[0], in_[0], Fn.Copy)], in_[1], out[1])
+
+    def act(out, in_, func, bias=0.0, scale=1.0, acc=None):
+        rd = list(in_[1])
+        wr = list(out[1])
+        bb = bias
+        if isinstance(bias, tuple):
+            rd += bias[1]
+            bb = bias[0]
+        if acc is not None:
+            wr += acc[1]
+            op("s", [lambda: g.scalar.activation(out[0], in_[0], func, bias=bb, scale=scale, accum_out=acc[0])], rd, wr)
+        else:
+            op("s", [lambda: g.scalar.activation(out[0], in_[0], func, bias=bb, scale=scale)], rd, wr)
+
+    def tt(out, a, b, o):
+        op("v", [lambda: g.vector.tensor_tensor(out[0], a[0], b[0], o)], a[1] + b[1], out[1])
+
+    def ts(out, a, s1, o1, s2=None, o2=None):
+        rd = list(a[1])
+        v = []
+        for s in (s1, s2):
+            if isinstance(s, tuple):
+                rd += s[1]
+                v.append(s[0])
+            else:
+                v.append(s)
+        if o2 is None:
+            op("v", [lambda: g.vector.tensor_scalar(out[0], a[0], v[0], None, o1)], rd, out[1])
+        else:
+            op("v", [lambda: g.vector.tensor_scalar(out[0], a[0], v[0], v[1], o1, o2)], rd, out[1])
+
+    def scan(out, d0, d1, init, o1, o2):
+        rd = d0[1] + d1[1]
+        ii = init
+        if isinstance(init, tuple):
+            rd = rd + init[1]
+            ii = init[0]
+        op("v", [lambda: g.vector.tensor_tensor_scan(out[0], d0[0], d1[0], ii, o1, o2)], rd, out[1])
+
+    def fill(reg, val):
+        op("v", [lambda: g.vector.memset(reg[0], val)], [], reg[1])
+
+    def mm(out, pairs, start=True, stop=True):
+        rd, fns = [], []
+        for k, (l, r) in enumerate(pairs):
+            rd += l[1] + r[1]
+            fns.append(lambda l=l, r=r, k=k: g.tensor.matmul(out[0], l[0], r[0], start and k == 0, stop and k == len(pairs) - 1))
+        op("p", fns, rd, out[1], not start)
+
+    def iota(reg, pattern, base, cm, flag):
+        if flag:
+            op("g", [lambda: g.iota(reg[0], pattern, base, cm, allow_small_or_imprecise_dtypes=True)], [], reg[1])
+        else:
+            op("g", [lambda: g.iota(reg[0], pattern, base, cm)], [], reg[1])
+
+    def asel(out, in_, pattern, cmp, base, cm):
+        op("g", [lambda: g.affine_select(out[0], in_[0], pattern, cmp, 0.0, base, cm)], in_[1], out[1])
+
+    dma("y", T.wtc[:], T.wt[:], [], [("wtc", 0, 1)])
+    dma("y", T.thc[:], T.th[:], [], [("thc", 0, 1)])
+    dma("y", T.X2[:, UP + S - G:UP + S], T.x0[:, S - G:S], [], [("X2", UP + S - G, UP + S)])
+    for a, b in ((0, 1024), (1024, S - G)):
+        dma("y", T.X2[:, UP + a:UP + b], T.x0[:, a:b], [], [("X2", UP + a, UP + b)])
+    for k in range(8):
+        dma("y", T.kdt[16 * k:16 * k + 16, :], T.kd[:], [], [("kdt", 0, U)], True)
+    dma("y", T.tac[:], T.tau[:], [], [("tac", 0, 1)])
+    dma("y", T.X2[:, 0:S], T.x0[:], [("kdt", 0, U)], [("X2", 0, S)])
+
+    fill(R("ones", 0, 128), 1.0)
+    iota(R("ci", 0, 1), [[0, 1]], 0, 1, False)
+    asel(R("blk2", 0, 128), R("ones", 0, 128), [[-16, 8], [0, 16]], Op.is_ge, 0, 1)
+    asel(R("blk", 0, 128), R("blk2", 0, 128), [[16, 8], [0, 16]], Op.is_ge, 15, -1)
+    asel(R("idp", 0, 128), R("ones", 0, 128), [[-1, 128]], Op.is_equal, 0, 1)
+    iota(R("k613", 0, 12), [[613 * 16, 12]], 0, 613, True)
+    asel(R("ida", 0, 128), R("ones", 0, 128), [[-1, 128]], Op.is_equal, 8, 1)
+    asel(R("idb", 0, 128), R("ones", 0, 128), [[-1, 128]], Op.is_equal, -8, 1)
+    iota(R("iof", 0, 512), [[1, 512]], 0, 0, True)
+    iota(R("iof", S, TOT), [[1, RO * G]], S, 0, True)
+
+    fill(R("wm", 0, 2048), 0.0)
+    fill(R("c14", 0, 512), 14.0)
+    flat = lambda nm, a, b, v: act(R(nm, a, b), R("c14", 0, b - a), Fn.Copy, bias=v, scale=0.0)
+    for a in range(0, 2048, 512):
+        flat("om", a, a + 512, 1.0)
+    om = R("om", 0, 2048)
+    asel(om, om, [[1, 16], [0, 8], [-1, 16]], Op.is_equal, 0, 0)
+    asel(om, om, [[0, 16], [-16, 8], [0, 16]], Op.is_ge, 0, 1)
+    asel(om, om, [[0, 16], [16, 8], [0, 16]], Op.is_ge, 15, -1)
+    iota(R("An", 0, RO * G), [[1, RO * G]], S, 0, True)
+    iota(R("iof4", 0, RO * G), [[1, RO * G]], S + 4096, 0, True)
+    flat("m8x", 0, 512, 1.0)
+    flat("m8n", 0, 512, 0.0)
+    for a in (0, 512):
+        flat("Wl", S + a, S + a + 512, 0.0)
+    ts(R("ci", 1, 2), R("ci", 0, 1), 15, Op.bitwise_and)
+    ts(R("ci", 2, 3), R("ci", 0, 1), 7, Op.bitwise_and)
+    ts(R("ci", 3, 4), R("ci", 0, 1), 4, Op.arith_shift_right)
+    ts(R("cf", 0, 1), R("ci", 1, 2), 8, Op.is_lt)
+    ts(R("cf", 1, 2), R("ci", 1, 2), 8, Op.is_ge)
+    ts(R("cf", 2, 3), R("ci", 1, 2), 0.5, Op.add)
+    ts(R("cf", 3, 4), R("ci", 1, 2), 16.5, Op.add)
+    ts(R("cf", 8, 9), R("ci", 2, 3), 0, Op.is_equal, float(TOT), Op.mult)
+    for t in range(RO):
+        ts(R("cf", 4 + t, 5 + t), R("cf", 8, 9), 128.0 * (10 + t) - 15.0 / 32, Op.add)
+    ts(R("pm", 0, 128), R("idp", 0, 128), R("cf", 0, 1), Op.mult)
+    ts(R("pm", 384, 512), R("idp", 0, 128), R("cf", 1, 2), Op.mult)
+    cp("v", R("id16", 0, 128), R("idp", 0, 128))
+    ts(R("idn", 0, 128), R("idp", 0, 128), -1.0, Op.mult)
+    cp("v", R("wtf", 0, 1), R("wtc", 0, 1))
+    for a in range(8):
+        ts(R("wm", 16 * a, 16 * a + 129 * 15 + 1, 129), R("blk", 16 * a, 16 * a + 16), R("wtf", 0, 1), Op.mult)
+    ts(R("cf", 9, 10), R("ci", 3, 4), -16.0 * 613, Op.mult)
+    ts(R("k613", 0, 12), R("k613", 0, 12), R("cf", 9, 10), Op.add)
+    cp("v", R("thf", 0, 1), R("thc", 0, 1))
+    ts(R("pm", 128, 256), R("ida", 0, 128), R("cf", 0, 1), Op.mult)
+    ts(R("pm", 256, 384), R("idb", 0, 128), R("cf", 1, 2), Op.mult)
+    bank = [("q0", 0), ("q1", 0), ("q2", 0), ("q3", 0), ("pD", 0)]
+    for b in range(5):
+        nm, o = bank[b]
+        ts(R("io16", 512 * b, 512 * b + 512), R("iof", 0, 512), 512.0 * b - (1792.0 if b == 4 else 0.0), Op.add)
+
+    def prepu(t):
+        src = ("X2", UP + S - G) if t == 0 else ("nxb", 0)
+        mm(R("pU", 0, 12), [(R("wm", 128 * p, 128 * p + 128), R(src[0], src[1] + p, src[1] + NP, 16)) for p in range(16)])
+
+    def prep(t):
+        tt(R("ui", 0, 12), R("pU", 0, 12), R("k613", 0, 12), Op.add)
+        ts(R("um", 0, 12), R("ui", 0, 12), U - 1, Op.bitwise_and)
+        cp("v", R("uo", 0, 12), R("um", 0, 12))
+
+    def kdg():
+        ts(R("ke", 0, NP), I("kdt", 0, U, "uo", 0, 12), -2048.0, Op.add)
+
+    def prep2(t):
+        ev, od = R("ke", 0, NP, 2), R("ke", 1, NP, 2)
+        mm(R("pU", 0, 96), [(R("pm", 0, 128), ev), (R("pm", 128, 256), od)])
+        mm(R("pU", 96, 192), [(R("pm", 256, 384), ev), (R("pm", 384, 512), od)])
+        sc, off = (10 + t) / 16.0, 128.0 * (10 + t) - 15.0 / 32
+        ts(R("tl1", 0, 96), R("pU", 0, 96), sc, Op.mult, R("cf", 4 + t, 5 + t), Op.add)
+        ts(R("th1", 0, 96), R("pU", 0, 96), sc, Op.mult, off, Op.add)
+        ts(R("t2", 0, 96), R("pU", 96, 192), sc, Op.mult, off, Op.add)
+
+    ts(R("idh", 0, 128), R("idp", 0, 128), 0.5, Op.mult)
+    fill(R("m8x", 0, 512, 8), 0.0)
+    fill(R("m8n", 0, 512, 8), 16384.0)
+    fill(R("onesr", 0, NP), 1.0)
+    fill(R("on16", 0, 128), 1.0 / 16)
+    fill(R("nxb", NP, 208), 0.0)
+    hb = ["pX", "pC"]
+    order = [0, 1, 2, 3, 4]
+    prepu(0)
+    for b in order:
+        nm, o = bank[b]
+        pr = [(R("id16", 0, 128), R("io16", 512 * b, 512 * b + 512))]
+        if b == 4:
+            pr.append((R("ones", 0, 128), R("c14", 0, 512)))
+        mm(R(nm, o, o + 512), pr)
+    prep(0)
+    for b in order:
+        a0, a1 = 512 * b, 512 * b + 512
+        ts(R("s8", a0, a1), R("X2", UP + a0, UP + a1), R("thf", 0, 1), Op.is_lt, 8192.0, Op.mult)
+        if b < 4:
+            act(R("s4", a0, a1), R("s8", a0, a1), Fn.Copy, scale=0.5)
+    for b in order:
+        a0, a1 = 512 * b, 512 * b + 512
+        pn = hb[b % 2]
+        mm(R(pn, 0, 512), [(R("id16", 0, 128), R("io16", a0, a1)), (R("idn", 0, 128), R("s8", a0, a1))])
+        act(R("Wh", a0, a1), R(pn, 0, 512), Fn.Identity, bias=4096.0 + (1792.0 if b == 4 else 0.0))
+    a0, a1 = 2048, 2560
+    mm(R("pC", 0, 512), [(R("id16", 0, 128), R("io16", a0, a1)), (R("idh", 0, 128), R("s8", a0, a1))])
+    act(R("Wl", TOT + a0, TOT + a1), R("pC", 0, 512), Fn.Identity, bias=1792.0)
+    for b in order:
+        a0, a1 = 512 * b, 512 * b + 512
+        nm, o = bank[b]
+        tt(R("Wl", a0, a1), R(nm, o, o + 512), R("s8", a0, a1), Op.add)
+        if b < 4:
+            tt(R("Wl", TOT + a0, TOT + a1), R(nm, o, o + 512), R("s4", a0, a1), Op.add)
+        if b == 3:
+            kdg()
+    fill(R("m16x", 0, 1024), 1.0)
+    fill(R("m16n", 0, 1024), 0.0)
+    fill(R("X2", S, UP), 0.0)
+    fill(R("m16x", 0, 1024, 16), 0.0)
+    fill(R("m16n", 0, 1024, 16), 512.0)
+    prep2(0)
+
+    cp("v", R("thr", 0, 1), R("tac", 0, 1))
+
+    starts = [sum(CHUNKS[:k]) for k in range(len(CHUNKS))]
+    nch = len(CHUNKS)
+    nloc = 0
+
+    for t in range(RO):
+        B = S + t * G
+
+        def first(c, wh, q, B=B):
+            i0, n = starts[c], CHUNKS[c]
+            w = (8 * i0, 8 * (i0 + n))
+            l = (i0 // 2, (i0 + n) // 2)
+            if wh == "l":
+                cp(q, R("L1", *w), I("Wl", 0, TOT + B, "tl1", *l))
+            else:
+                cp(q, R("H1", *w), I("Wh", 0, B, "th1", *l))
+
+        def g1v(c, B=B):
+            i0, n = starts[c], CHUNKS[c]
+            w = (8 * i0, 8 * (i0 + n))
+            l = (i0 // 2, (i0 + n) // 2)
+            tt(R("al", *w), I("Wl", 0, TOT + B, "t2", *l), R("L1", *w), Op.min)
+            tt(R("ah", *w), I("Wh", 0, B, "t2", *l), R("H1", *w), Op.max)
+            scan(R("sl", *w), R("m8n", 0, 8 * n), R("al", *w), 0.0, Op.max, Op.min)
+            cp("v", R("ol", i0, i0 + n), R("sl", 8 * i0 + 7, 8 * (i0 + n), 8))
+            scan(R("sh", *w), R("m8x", 0, 8 * n), R("ah", *w), 0.0, Op.mult, Op.max)
+            tt(R("hc", i0, i0 + n), R("sh", 8 * i0 + 7, 8 * (i0 + n), 8), R("sl", 8 * i0 + 7, 8 * (i0 + n), 8), Op.max)
+            ts(R("oh", i0, i0 + n), R("hc", i0, i0 + n), -4096.0, Op.add)
+
+        def second(c, wh, q, B=B):
+            i0, n = starts[c], CHUNKS[c]
+            if wh == "XL":
+                cp(q, R("XL", 16 * i0, 16 * (i0 + n)), I("X2", 0, UP + B, "ol", i0, i0 + n))
+            else:
+                cp(q, R("XH", 16 * i0, 16 * (i0 + n)), I("X2", UP, UP + B, "oh", i0, i0 + n))
+
+        def blocks(c):
+            i0, n = starts[c], CHUNKS[c]
+            nb = sum((16 * m + 511) // 512 for m in CHUNKS[:c])
+            return [("q%d" % ((nb + k) % 4), 16 * i0 + a, 16 * i0 + min(a + 512, 16 * n)) for k, a in enumerate(range(0, 16 * n, 512))]
+
+        def diff(c, part):
+            for pn, a, e in blocks(c):
+                mm(R(pn, 0, e - a), [(R(("idp", "idn")[part], 0, 128), R(("XL", "XH")[part], a, e))], part == 0, part == 1)
+
+        def absd(c):
+            for pn, a, e in blocks(c):
+                act(R("ad", a, e), R(pn, 0, e - a), Fn.Abs)
+
+        def dsum(c):
+            i0, n = starts[c], CHUNKS[c]
+            mm(R("pD" if c % 2 == 0 else "pX", i0, i0 + n), [(R("om", 128 * p, 128 * p + 128), R("ad", 16 * i0 + p, 16 * (i0 + n), 16)) for p in range(16)])
+
+        def farv(c):
+            i0, n = starts[c], CHUNKS[c]
+            ts(R("far", i0, i0 + n), R("pD" if c % 2 == 0 else "pX", i0, i0 + n), R("thr", 0, 1), Op.is_gt)
+
+        def cntp(c):
+            i0, n = starts[c], CHUNKS[c]
+            mm(R("pC", i0, i0 + n), [(R("blk", 0, 128), R("far", i0, i0 + n))])
+
+        def cumv(c):
+            i0, n = starts[c], CHUNKS[c]
+            ts(R("flg", i0, i0 + n), R("pC", i0, i0 + n), 0.0, Op.is_gt)
+            scan(R("cum", i0, i0 + n), R("onesr", i0, i0 + n), R("flg", i0, i0 + n), 0.0 if c == 0 else R("cum", i0 - 1, i0), Op.mult, Op.add)
+
+        def nxv(c):
+            i0, n = starts[c], CHUNKS[c]
+            w = (16 * i0, 16 * (i0 + n))
+            last = (16 * i0 + 15, 16 * (i0 + n), 16)
+            scan(R("mxs", *w), R("m16x", 0, 16 * n), R("XL", *w), 0.0, Op.mult, Op.max)
+            scan(R("mns", *w), R("m16n", 0, 16 * n), R("XH", *w), 0.0, Op.max, Op.min)
+            tt(R("sm", i0, i0 + n), R("mxs", *last), R("mns", *last), Op.add)
+            ts(R("si", i0, i0 + n), R("sm", i0, i0 + n), 0.5, Op.mult, -0.25, Op.add)
+            cp("v", R("nxb", i0, i0 + n), R("si", i0, i0 + n))
+
+        steps = {"l": lambda c: first(c, "l", "s"), "h": lambda c: first(c, "h", "s"), "H": lambda c: first(c, "h", "v"),
+                 "a": g1v, "x": lambda c: second(c, "XL", "s"), "y": lambda c: second(c, "XH", "s"),
+                 "Y": lambda c: second(c, "XH", "v"), "e": lambda c: diff(c, 0), "d": lambda c: diff(c, 1), "b": absd, "D": dsum,
+                 "f": farv, "k": cntp, "c": cumv, "n": nxv}
+        for st in ORDER.split():
+            steps[st[0]](int(st[1:]))
+
+        for h in range(2):
+            act(R("sg", h * NP, h * NP + NP), R("cum", 0, NP), Fn.Sign, bias=R("cf", 2 + h, 3 + h), scale=-1.0, acc=R("cnt2", h, h + 1))
+        if t + 1 < RO:
+            prepu(t + 1)
+        ts(R("mo", 0, 2), R("cnt2", 0, 2), 0.5, Op.mult, 96.0, Op.add)
+        cp("v", R("mailb", t * CAP, (t + 1) * CAP), I("nxb", 0, 208, "mo", 0, 2))
+        direct, via = plan[rank, t]
+        ml = T.mailb[:, t * CAP:(t + 1) * CAP]
+        dowait("g", need("g", [("mailb", t * CAP, (t + 1) * CAP)], []))
+        tr = []
+        if via:
+            ids = []
+            for rc in relay[rank][:len(via)]:
+                rid, pid = topo.addr(rc, core)
+                ids.append(DstId(rid=rid, pnc=pid))
+            m, k = emask(topo, core, relay[rank][0], True, not direct)
+            nloc += k
+            tr.append(RemoteDMATransfer(dst_ids=ids, dma_engine_mask=m, remote_sem=T.sem["rl%d" % t], srcs=[ml],
+                                        dsts=[T.rbuf[:, t * CAP:(t + 1) * CAP] for rc in ids]))
+        if direct:
+            ids, outs = [], []
+            for f, d in direct:
+                rid, pid = topo.addr(d, core)
+                ids.append(DstId(rid=rid, pnc=pid))
+                a, b = land(t, f)
+                outs.append(T.X2[:, a:b])
+            m, k = emask(topo, core, direct[0][1], False)
+            nloc += k
+            tr.append(RemoteDMATransfer(dst_ids=ids, dma_engine_mask=m, remote_sem=T.sem["ar%d" % t], srcs=[ml], dsts=outs))
+        g.remote_dma_fused(tr, local_sem=T.sem.loc)
+
+        cp("s", R("X2", UP + B, UP + B + NP), R("nxb", 0, NP))
+        if t + 1 < RO:
+            prep(t + 1)
+            kdg()
+            prep2(t + 1)
+            cp("s", R("X2", B, B + NP), R("nxb", 0, NP))
+        mn = R("sl", 7, 1536, 8)
+        ts(R("lq", 0, NP), mn, 4096.0, Op.is_ge, -4096.0, Op.mult)
+        tt(R("lt", 0, NP), mn, R("lq", 0, NP), Op.add)
+        tt(R("fi", 0, NP), R("far", 0, NP), R("iof", B, B + NP), Op.mult)
+        j0 = t * G
+        tt(R("An", j0, j0 + NP), R("lt", 0, NP), R("fi", 0, NP), Op.max)
+        dma("y", T.ya[:, j0:j0 + G], T.An[:, j0:j0 + G], [("An", j0, j0 + G)], [])
+        dma("y", T.yx[:, j0:j0 + NP], T.X2[:, UP + B:UP + B + NP], [("X2", UP + B, UP + B + NP)], [])
+
+        def window(a0, a1, names, names4):
+            w = a1 - a0
+            e = a0 - B
+            ts(R("e8", e, e + w), R("X2", UP + a0, UP + a1), R("thf", 0, 1), Op.is_lt, 8192.0, Op.mult)
+            ts(R("e4", e, e + w), R("X2", UP + a0, UP + a1), R("thf", 0, 1), Op.is_lt, 4096.0, Op.mult)
+            tt(R("Wl", a0, a1), names, R("e8", e, e + w), Op.add)
+            tt(R("Wl", TOT + a0, TOT + a1), names, R("e4", e, e + w), Op.add)
+            tt(R("Wh", a0, a1), names4, R("e8", e, e + w), Op.subtract)
+
+        if t + 1 < RO:
+            mm(R("pC", 256, 257), [(R("on16", 0, 128), R("cum", NP - 1, NP))])
+            cp("v", R("cci", 0, 1), R("pC", 256, 257))
+            ts(R("cci", 1, 2), R("cci", 0, 1), 15, Op.bitwise_and)
+            tt(R("thr", 0, 1), R("cci", 1, 2), R("tac", 0, 1), Op.add)
+            ts(R("a4", 0, NP), R("An", j0, j0 + NP), 4096.0, Op.add)
+            window(B, B + NP, R("An", j0, j0 + NP), R("a4", 0, NP))
+
+        key = "ar%d" % t
+        narr = 0
+        for f in range(FO):
+            s = T.cores[(rank - 1 - ((FO * t + f) % (len(T.cores) - 1))) % len(T.cores)]
+            if not topo.may_write(s, core):
+                s = relay[T.rank_of(s)][0]
+            narr += emask(topo, s, core, False)[1]
+        semof[key] = T.sem[key]
+        clock[key, narr] = {}
+        note(key, narr, [], [("X2", UP + B + NP, UP + B + G)])
+        if t + 1 < RO:
+            window(B + NP, B + G, R("iof", B + NP, B + G), R("iof4", j0 + NP, j0 + G))
+            cp("s", R("X2", B + NP, B + G), R("X2", UP + B + NP, UP + B + G))
+        dma("y", T.yx[:, j0 + NP:j0 + G], T.X2[:, UP + B + NP:UP + B + G], [("X2", UP + B + NP, UP + B + G)], [])
+
+    g.wait_ge(T.sem.loc, nloc)
+    for q in ("v", "s", "p", "g"):
+        g.wait_ge(semof[q], count[q])
+    for k in range(ndma[0]):
+        g.wait_ge(T.sem["d%d" % k], 16)

@@ -4,21 +4,28 @@ from concourse.mybir import AluOpType as Op, ActivationFunctionType as Fn
 S, U, NP, CAP, FO, RO = 2560, 2048, 192, 32, 2, 4
 G = NP + FO * CAP
 TOT = S + RO * G
-UP = 4096
+K = 8192.0
+MID = 2048
+RND = 12582912.0
 CHUNKS = [64, 64, 64]
-ORDER = "l0 l1 H0 a0 l2 h1 x0 e0 Y0 a1 d0 h2 b0 x1 e1 y1 n0 d1 a2 D0 Y2 b1 D1 x2 e2 n2 d2 f1 b2 f0 k0 k1 D2 n1 c0 c1 f2 k2 c2"
+ORDER = ("l0 H0 c0 l1 A0 B0 h1 s0 t0 c1 p0 q0 r0 l2 u0 v0 x0 A1 B1 c2 y0 e0 s1 t1 d0 p1 q1 r1 u1 v1 H2 A2 B2 x1 b0 s2 t2 p2 q2 r2 u2 v2 "
+         "y1 e1 D0 m0 n0 d1 x2 Y2 a0 b1 e2 m1 n1 d2 w0 a1 D1 b2 m2 w1 n2 f0 f1 a2 D2 k0 k1 w2 g0 g1 f2 k2 j0 j1 g2 j2")
 
 SCRATCH = {
-    "X2": ("sbuf", [128, UP + TOT], "bfloat16"),
-    "Wl": ("sbuf", [128, 2 * TOT], "float32"),
+    "X": ("sbuf", [128, TOT], "bfloat16"),
+    "Wl": ("sbuf", [128, TOT], "float32"),
     "Wh": ("sbuf", [128, TOT], "float32"),
-    "kdt": ("sbuf", [128, U], "int32"),
-    "iof": ("sbuf", [128, TOT], "float32"),
-    "io16": ("sbuf", [128, S], "float16"),
-    "c14": ("sbuf", [128, 512], "bfloat16"),
+    "kq": ("sbuf", [128, 256], "int32"),
+    "k16": ("sbuf", [128, 256], "float16"),
+    "ksel": ("sbuf", [128, 1024], "bfloat16"),
+    "kdt": ("sbuf", [128, U], "float32"),
+    "ones": ("sbuf", [128, 1024], "bfloat16"),
+    "io16": ("sbuf", [128, 512], "float16"),
+    "ib": ("sbuf", [128, 128], "bfloat16"),
+    "cm": ("sbuf", [128, 384], "bfloat16"),
     "s8": ("sbuf", [128, S], "bfloat16"),
-    "s4": ("sbuf", [128, S], "bfloat16"),
     "An": ("sbuf", [128, RO * G], "float32"),
+    "iom": ("sbuf", [128, RO * FO * CAP], "float32"),
     "ci": ("sbuf", [128, 16], "int32"),
     "cf": ("sbuf", [128, 16], "float32"),
     "k613": ("sbuf", [128, 12], "float32"),
@@ -29,14 +36,11 @@ SCRATCH = {
     "thf": ("sbuf", [128, 1], "float32"),
     "thr": ("sbuf", [128, 1], "float32"),
     "cci": ("sbuf", [128, 2], "int32"),
-    "ones": ("sbuf", [128, 128], "bfloat16"),
     "blk": ("sbuf", [128, 128], "bfloat16"),
-    "blk2": ("sbuf", [128, 128], "bfloat16"),
     "idp": ("sbuf", [128, 128], "bfloat16"),
     "idn": ("sbuf", [128, 128], "bfloat16"),
     "idh": ("sbuf", [128, 128], "bfloat16"),
-    "ida": ("sbuf", [128, 128], "bfloat16"),
-    "idb": ("sbuf", [128, 128], "bfloat16"),
+    "idk": ("sbuf", [128, 128], "bfloat16"),
     "on16": ("sbuf", [128, 128], "bfloat16"),
     "id16": ("sbuf", [128, 128], "float16"),
     "pm": ("sbuf", [128, 512], "float16"),
@@ -46,21 +50,22 @@ SCRATCH = {
     "m8n": ("sbuf", [128, 512], "bfloat16"),
     "m16x": ("sbuf", [128, 1024], "bfloat16"),
     "m16n": ("sbuf", [128, 1024], "bfloat16"),
-    "onesr": ("sbuf", [128, NP], "bfloat16"),
     "ui": ("sbuf", [128, 12], "int32"),
     "um": ("sbuf", [128, 12], "int32"),
     "uo": ("sbuf", [128, 12], "uint16"),
     "ke": ("sbuf", [128, NP], "float16"),
-    "tl1": ("sbuf", [128, 96], "uint16"),
-    "th1": ("sbuf", [128, 96], "uint16"),
+    "t1": ("sbuf", [128, 96], "uint16"),
     "t2": ("sbuf", [128, 96], "uint16"),
     "L1": ("sbuf", [128, 1536], "float32"),
     "H1": ("sbuf", [128, 1536], "float32"),
-    "al": ("sbuf", [128, 1536], "float32"),
-    "ah": ("sbuf", [128, 1536], "float32"),
-    "sl": ("sbuf", [128, 1536], "float32"),
-    "sh": ("sbuf", [128, 1536], "float32"),
-    "hc": ("sbuf", [128, NP], "float32"),
+    "al": ("sbuf", [128, 1536], "float16"),
+    "ah": ("sbuf", [128, 1536], "float16"),
+    "sl": ("sbuf", [128, 1536], "float16"),
+    "sh": ("sbuf", [128, 1536], "float16"),
+    "c0": ("sbuf", [128, NP], "float32"),
+    "yy": ("sbuf", [128, NP], "float16"),
+    "lo": ("sbuf", [128, NP], "float16"),
+    "hi": ("sbuf", [128, NP], "float16"),
     "ol": ("sbuf", [128, NP], "uint16"),
     "oh": ("sbuf", [128, NP], "uint16"),
     "XL": ("sbuf", [128, 3072], "bfloat16"),
@@ -68,10 +73,8 @@ SCRATCH = {
     "ad": ("sbuf", [128, 3072], "bfloat16"),
     "mxs": ("sbuf", [128, 3072], "bfloat16"),
     "mns": ("sbuf", [128, 3072], "bfloat16"),
-    "sm": ("sbuf", [128, NP], "float32"),
-    "si": ("sbuf", [128, NP], "int32"),
     "nxb": ("sbuf", [128, 208], "bfloat16"),
-    "far": ("sbuf", [128, NP], "bfloat16"),
+    "near": ("sbuf", [128, NP], "bfloat16"),
     "flg": ("sbuf", [128, NP], "bfloat16"),
     "cum": ("sbuf", [128, NP], "bfloat16"),
     "sg": ("sbuf", [128, 2 * NP], "bfloat16"),
@@ -79,13 +82,8 @@ SCRATCH = {
     "mo": ("sbuf", [128, 2], "uint16"),
     "mailb": ("sbuf", [128, RO * CAP], "bfloat16"),
     "rbuf": ("sbuf", [128, RO * CAP], "bfloat16"),
-    "lq": ("sbuf", [128, NP], "float32"),
-    "lt": ("sbuf", [128, NP], "float32"),
-    "fi": ("sbuf", [128, NP], "float32"),
-    "a4": ("sbuf", [128, NP], "float32"),
+    "A16": ("sbuf", [128, NP], "float16"),
     "e8": ("sbuf", [128, G], "bfloat16"),
-    "e4": ("sbuf", [128, G], "bfloat16"),
-    "iof4": ("sbuf", [128, RO * G], "float32"),
     "q0": ("psum", [128, 512], "float32"),
     "q1": ("psum", [128, 512], "float32"),
     "q2": ("psum", [128, 512], "float32"),
@@ -96,7 +94,7 @@ SCRATCH = {
     "pU": ("psum", [128, 512], "float32"),
 }
 PSUM = ("q0", "q1", "q2", "q3", "pD", "pX", "pC", "pU")
-NDMA = 40
+NDMA = 24
 SEMAPHORES = (["sv", "ss", "sp", "sg", "loc"] + ["ar%d" % t for t in range(RO)] + ["rl%d" % t for t in range(RO)]
               + ["d%d" % i for i in range(NDMA)])
 
@@ -125,7 +123,7 @@ def emask(topo, src, dst, high, full=False):
 
 
 def land(t, f):
-    b = UP + S + t * G + NP + f * CAP
+    b = S + t * G + NP + f * CAP
     return b, b + CAP
 
 
@@ -143,7 +141,7 @@ def relay_program(g, core, T, topo, r, which, plan):
             rid, pid = topo.addr(d, core)
             ids.append(DstId(rid=rid, pnc=pid))
             a, b = land(t, f)
-            outs.append(T.X2[:, a:b])
+            outs.append(T.X[:, a:b])
         g.remote_dma_fused([RemoteDMATransfer(dst_ids=ids, dma_engine_mask=m, remote_sem=T.sem["ar%d" % t],
                                               srcs=[T.rbuf[:, t * CAP:(t + 1) * CAP]], dsts=outs)], local_sem=T.sem.loc)
         sent += k
@@ -212,9 +210,8 @@ def rank_program(g, core, T, topo):
             clock[q, count[q]] = dict(known[q])
         note(q, count[q], reads, writes)
 
-    def dma(q, out, in_, reads, writes, alone=False):
-        if not alone:
-            dowait(q, need(q, reads, writes))
+    def dma(q, out, in_, reads, writes):
+        dowait(q, need(q, reads, writes))
         key = "d%d" % ndma[0]
         ndma[0] += 1
         semof[key] = T.sem[key]
@@ -222,14 +219,11 @@ def rank_program(g, core, T, topo):
         clock[key, 16] = dict(known[q])
         note(key, 16, reads, writes)
 
-    def R(name, a, b, step=1):
-        return (T[name][:, a:b:step] if step != 1 else T[name][:, a:b], [(name, a, b)])
+    def R(name, a, b, step=1, rows=128):
+        return (T[name][0:rows, a:b:step] if step != 1 else T[name][0:rows, a:b], [(name, a, b)])
 
     def I(win, a, b, off, c, d):
         return (T[win][:, a:b].indirect(T[off][:, c:d]), [(win, a, b), (off, c, d)])
-
-    def col(name, j):
-        return R(name, j, j + 1)
 
     def cp(q, out, in_):
         if q == "v":
@@ -285,7 +279,7 @@ def rank_program(g, core, T, topo):
             fns.append(lambda l=l, r=r, k=k: g.tensor.matmul(out[0], l[0], r[0], start and k == 0, stop and k == len(pairs) - 1))
         op("p", fns, rd, out[1], not start)
 
-    def iota(reg, pattern, base, cm, flag):
+    def iota(reg, pattern, base, cm, flag=True):
         if flag:
             op("g", [lambda: g.iota(reg[0], pattern, base, cm, allow_small_or_imprecise_dtypes=True)], [], reg[1])
         else:
@@ -294,223 +288,228 @@ def rank_program(g, core, T, topo):
     def asel(out, in_, pattern, cmp, base, cm):
         op("g", [lambda: g.affine_select(out[0], in_[0], pattern, cmp, 0.0, base, cm)], in_[1], out[1])
 
+    def M(name, j=0):
+        return R(name, 128 * j, 128 * j + 128)
+
+    def C(j):
+        return R("cf", j, j + 1)
+
+    def shift(n, w):
+        k = abs(n) // 16
+        return (R("cm", 0 if n < 0 else 128, 128 if n < 0 else 256, 1, k), R("ones", 0, w, 1, k))
+
     dma("y", T.wtc[:], T.wt[:], [], [("wtc", 0, 1)])
-    dma("y", T.thc[:], T.th[:], [], [("thc", 0, 1)])
-    dma("y", T.X2[:, UP + S - G:UP + S], T.x0[:, S - G:S], [], [("X2", UP + S - G, UP + S)])
-    for a, b in ((0, 1024), (1024, S - G)):
-        dma("y", T.X2[:, UP + a:UP + b], T.x0[:, a:b], [], [("X2", UP + a, UP + b)])
-    for k in range(8):
-        dma("y", T.kdt[16 * k:16 * k + 16, :], T.kd[:], [], [("kdt", 0, U)], True)
+    dma("s", T.X[:, 2048:S], T.x0[:, 2048:S], [], [("X", 2048, S)])
+    dma("y", T.kq[:], T.kd[:], [], [("kq", 0, 256)])
+    dma("s", T.thc[:], T.th[:], [], [("thc", 0, 1)])
+    dma("y", T.X[:, 0:1024], T.x0[:, 0:1024], [], [("X", 0, 1024)])
+    dma("s", T.X[:, 1024:2048], T.x0[:, 1024:2048], [], [("X", 1024, 2048)])
     dma("y", T.tac[:], T.tau[:], [], [("tac", 0, 1)])
-    dma("y", T.X2[:, 0:S], T.x0[:], [("kdt", 0, U)], [("X2", 0, S)])
 
-    fill(R("ones", 0, 128), 1.0)
+    fill(R("ones", 0, 1024), 1.0)
     iota(R("ci", 0, 1), [[0, 1]], 0, 1, False)
-    asel(R("blk2", 0, 128), R("ones", 0, 128), [[-16, 8], [0, 16]], Op.is_ge, 0, 1)
-    asel(R("blk", 0, 128), R("blk2", 0, 128), [[16, 8], [0, 16]], Op.is_ge, 15, -1)
-    asel(R("idp", 0, 128), R("ones", 0, 128), [[-1, 128]], Op.is_equal, 0, 1)
-    iota(R("k613", 0, 12), [[613 * 16, 12]], 0, 613, True)
-    asel(R("ida", 0, 128), R("ones", 0, 128), [[-1, 128]], Op.is_equal, 8, 1)
-    asel(R("idb", 0, 128), R("ones", 0, 128), [[-1, 128]], Op.is_equal, -8, 1)
-    iota(R("iof", 0, 512), [[1, 512]], 0, 0, True)
-    iota(R("iof", S, TOT), [[1, RO * G]], S, 0, True)
-
+    iota(R("ib", 0, 128), [[1, 8], [0, 16]], 0, 0)
+    asel(R("ksel", 0, 1024), R("ones", 0, 1024), [[-1, 8], [0, 8], [-8, 16]], Op.is_equal, 0, 1)
+    iota(R("k613", 0, 12), [[613 * 16, 12]], 0, 0)
     fill(R("wm", 0, 2048), 0.0)
-    fill(R("c14", 0, 512), 14.0)
-    flat = lambda nm, a, b, v: act(R(nm, a, b), R("c14", 0, b - a), Fn.Copy, bias=v, scale=0.0)
-    for a in range(0, 2048, 512):
-        flat("om", a, a + 512, 1.0)
-    om = R("om", 0, 2048)
-    asel(om, om, [[1, 16], [0, 8], [-1, 16]], Op.is_equal, 0, 0)
-    asel(om, om, [[0, 16], [-16, 8], [0, 16]], Op.is_ge, 0, 1)
-    asel(om, om, [[0, 16], [16, 8], [0, 16]], Op.is_ge, 15, -1)
-    iota(R("An", 0, RO * G), [[1, RO * G]], S, 0, True)
-    iota(R("iof4", 0, RO * G), [[1, RO * G]], S + 4096, 0, True)
-    flat("m8x", 0, 512, 1.0)
-    flat("m8n", 0, 512, 0.0)
-    for a in (0, 512):
-        flat("Wl", S + a, S + a + 512, 0.0)
+    scan(R("io16", 0, 512), R("ones", 0, 512), R("ones", 0, 512), -1.0, Op.mult, Op.add)
     ts(R("ci", 1, 2), R("ci", 0, 1), 15, Op.bitwise_and)
-    ts(R("ci", 2, 3), R("ci", 0, 1), 7, Op.bitwise_and)
-    ts(R("ci", 3, 4), R("ci", 0, 1), 4, Op.arith_shift_right)
-    ts(R("cf", 0, 1), R("ci", 1, 2), 8, Op.is_lt)
-    ts(R("cf", 1, 2), R("ci", 1, 2), 8, Op.is_ge)
-    ts(R("cf", 2, 3), R("ci", 1, 2), 0.5, Op.add)
-    ts(R("cf", 3, 4), R("ci", 1, 2), 16.5, Op.add)
-    ts(R("cf", 8, 9), R("ci", 2, 3), 0, Op.is_equal, float(TOT), Op.mult)
-    for t in range(RO):
-        ts(R("cf", 4 + t, 5 + t), R("cf", 8, 9), 128.0 * (10 + t) - 15.0 / 32, Op.add)
-    ts(R("pm", 0, 128), R("idp", 0, 128), R("cf", 0, 1), Op.mult)
-    ts(R("pm", 384, 512), R("idp", 0, 128), R("cf", 1, 2), Op.mult)
-    cp("v", R("id16", 0, 128), R("idp", 0, 128))
-    ts(R("idn", 0, 128), R("idp", 0, 128), -1.0, Op.mult)
+    ts(R("ci", 2, 3), R("ci", 0, 1), 4, Op.arith_shift_right)
+    cp("v", C(0), R("ci", 0, 1))
+    fill(M("cm", 0), -16.0)
+    cp("v", C(1), R("ci", 2, 3))
+    ts(C(2), R("ci", 1, 2), 613.0, Op.mult)
+    io = R("io16", 0, 128)
+    ts(M("id16"), io, C(0), Op.is_equal)
+    ts(M("blk"), M("ib"), C(1), Op.is_equal)
+    ts(M("idn"), io, C(0), Op.is_equal, -1.0, Op.mult)
+    ts(M("idp"), io, C(0), Op.is_equal)
+    for b in range(4):
+        mm(R("q%d" % b, 0, 512), [(M("id16"), R("io16", 0, 512)), shift(512 * b - MID, 512)])
     cp("v", R("wtf", 0, 1), R("wtc", 0, 1))
+    ts(R("k16", 0, 256), R("kq", 0, 256), -2048.0, Op.add)
     for a in range(8):
         ts(R("wm", 16 * a, 16 * a + 129 * 15 + 1, 129), R("blk", 16 * a, 16 * a + 16), R("wtf", 0, 1), Op.mult)
-    ts(R("cf", 9, 10), R("ci", 3, 4), -16.0 * 613, Op.mult)
-    ts(R("k613", 0, 12), R("k613", 0, 12), R("cf", 9, 10), Op.add)
-    cp("v", R("thf", 0, 1), R("thc", 0, 1))
-    ts(R("pm", 128, 256), R("ida", 0, 128), R("cf", 0, 1), Op.mult)
-    ts(R("pm", 256, 384), R("idb", 0, 128), R("cf", 1, 2), Op.mult)
-    bank = [("q0", 0), ("q1", 0), ("q2", 0), ("q3", 0), ("pD", 0)]
-    for b in range(5):
-        nm, o = bank[b]
-        ts(R("io16", 512 * b, 512 * b + 512), R("iof", 0, 512), 512.0 * b - (1792.0 if b == 4 else 0.0), Op.add)
+    iota(R("m8n", 0, 512), [[0, 64], [-20480, 8]], 16384, 0)
+    iota(R("m8x", 0, 512), [[0, 64], [20480, 8]], -16384, 0)
+    iota(R("om", 0, 2048), [[0, 2048]], 0, 0)
+    for a in range(8):
+        asel(R("om", 16 * a, 16 * a + 129 * 15 + 1, 129), R("blk", 16 * a, 16 * a + 16), [[0, 16]], Op.is_ge, 0, 0)
+    iota(R("m16x", 0, 1024), [[0, 64], [256, 16]], 0, 0)
+    iota(R("m16n", 0, 1024), [[0, 64], [-256, 16]], 256, 0)
+    iota(R("iom", 0, RO * FO * CAP), [[G, RO], [1, FO * CAP]], S + NP - MID, 0)
+    iota(R("An", 0, RO * G), [[1, RO * G]], S, 0)
 
     def prepu(t):
-        src = ("X2", UP + S - G) if t == 0 else ("nxb", 0)
-        mm(R("pU", 0, 12), [(R("wm", 128 * p, 128 * p + 128), R(src[0], src[1] + p, src[1] + NP, 16)) for p in range(16)])
+        src = ("X", S - G) if t == 0 else ("nxb", 0)
+        mm(R("pU", 0, 12), [(M("wm", p), R(src[0], src[1] + p, src[1] + NP, 16)) for p in range(16)])
 
-    def prep(t):
+    def prep():
         tt(R("ui", 0, 12), R("pU", 0, 12), R("k613", 0, 12), Op.add)
+        yield
         ts(R("um", 0, 12), R("ui", 0, 12), U - 1, Op.bitwise_and)
+        yield
         cp("v", R("uo", 0, 12), R("um", 0, 12))
-
-    def kdg():
-        ts(R("ke", 0, NP), I("kdt", 0, U, "uo", 0, 12), -2048.0, Op.add)
+        yield
+        cp("v", R("ke", 0, NP), I("kdt", 0, U, "uo", 0, 12))
+        ev, od = R("ke", 0, NP, 2), R("ke", 1, NP, 2)
+        mm(R("pU", 0, 96), [(M("pm", 0), ev), (M("pm", 1), od)])
+        mm(R("pU", 96, 192), [(M("pm", 2), ev), (M("pm", 3), od)])
+        yield
 
     def prep2(t):
-        ev, od = R("ke", 0, NP, 2), R("ke", 1, NP, 2)
-        mm(R("pU", 0, 96), [(R("pm", 0, 128), ev), (R("pm", 128, 256), od)])
-        mm(R("pU", 96, 192), [(R("pm", 256, 384), ev), (R("pm", 384, 512), od)])
         sc, off = (10 + t) / 16.0, 128.0 * (10 + t) - 15.0 / 32
-        ts(R("tl1", 0, 96), R("pU", 0, 96), sc, Op.mult, R("cf", 4 + t, 5 + t), Op.add)
-        ts(R("th1", 0, 96), R("pU", 0, 96), sc, Op.mult, off, Op.add)
+        ts(R("t1", 0, 96), R("pU", 0, 96), sc, Op.mult, off, Op.add)
         ts(R("t2", 0, 96), R("pU", 96, 192), sc, Op.mult, off, Op.add)
 
-    ts(R("idh", 0, 128), R("idp", 0, 128), 0.5, Op.mult)
-    fill(R("m8x", 0, 512, 8), 0.0)
-    fill(R("m8n", 0, 512, 8), 16384.0)
-    fill(R("onesr", 0, NP), 1.0)
-    fill(R("on16", 0, 128), 1.0 / 16)
-    fill(R("nxb", NP, 208), 0.0)
-    hb = ["pX", "pC"]
-    order = [0, 1, 2, 3, 4]
-    prepu(0)
-    for b in order:
-        nm, o = bank[b]
-        pr = [(R("id16", 0, 128), R("io16", 512 * b, 512 * b + 512))]
-        if b == 4:
-            pr.append((R("ones", 0, 128), R("c14", 0, 512)))
-        mm(R(nm, o, o + 512), pr)
-    prep(0)
-    for b in order:
-        a0, a1 = 512 * b, 512 * b + 512
-        ts(R("s8", a0, a1), R("X2", UP + a0, UP + a1), R("thf", 0, 1), Op.is_lt, 8192.0, Op.mult)
-        if b < 4:
-            act(R("s4", a0, a1), R("s8", a0, a1), Fn.Copy, scale=0.5)
-    for b in order:
-        a0, a1 = 512 * b, 512 * b + 512
-        pn = hb[b % 2]
-        mm(R(pn, 0, 512), [(R("id16", 0, 128), R("io16", a0, a1)), (R("idn", 0, 128), R("s8", a0, a1))])
-        act(R("Wh", a0, a1), R(pn, 0, 512), Fn.Identity, bias=4096.0 + (1792.0 if b == 4 else 0.0))
-    a0, a1 = 2048, 2560
-    mm(R("pC", 0, 512), [(R("id16", 0, 128), R("io16", a0, a1)), (R("idh", 0, 128), R("s8", a0, a1))])
-    act(R("Wl", TOT + a0, TOT + a1), R("pC", 0, 512), Fn.Identity, bias=1792.0)
-    for b in order:
-        a0, a1 = 512 * b, 512 * b + 512
-        nm, o = bank[b]
-        tt(R("Wl", a0, a1), R(nm, o, o + 512), R("s8", a0, a1), Op.add)
-        if b < 4:
-            tt(R("Wl", TOT + a0, TOT + a1), R(nm, o, o + 512), R("s4", a0, a1), Op.add)
-        if b == 3:
-            kdg()
-    fill(R("m16x", 0, 1024), 1.0)
-    fill(R("m16n", 0, 1024), 0.0)
-    fill(R("X2", S, UP), 0.0)
-    fill(R("m16x", 0, 1024, 16), 0.0)
-    fill(R("m16n", 0, 1024, 16), 512.0)
-    prep2(0)
+    rot = ["pD", "pX", "pC"]
+    for b in range(4):
+        for h in range(2):
+            mm(R(rot[b % 3], 256 * h, 256 * h + 256), [(M("ksel", 2 * b + h), R("k16", 0, 256))])
+        if b == 1:
+            prepu(0)
+        cp("s" if b != 1 else "v", R("kdt", 512 * b, 512 * b + 512), R(rot[b % 3], 0, 512))
+    cp("v", R("thf", 0, 1), R("thc", 0, 1))
+    ts(R("k613", 0, 12), R("k613", 0, 12), C(2), Op.add)
+    ts(C(3), R("ci", 1, 2), 8, Op.is_lt)
+    ts(C(4), R("ci", 1, 2), 8, Op.is_ge)
+    ts(C(5), C(0), 8.0, Op.add)
+    ts(C(6), C(0), -8.0, Op.add)
 
+    def s8(b):
+        ts(R("s8", 512 * b, 512 * b + 512), R("X", 512 * b, 512 * b + 512), R("thf", 0, 1), Op.is_lt, K, Op.mult)
+
+    nrot = [1]
+
+    def code(win, b):
+        pn = rot[nrot[0] % 3]
+        nrot[0] += 1
+        mm(R(pn, 0, 512), [(M("id16"), R("io16", 0, 512)), (M("idp" if win == "Wl" else "idn"), R("s8", 512 * b, 512 * b + 512))])
+        act(R(win, 512 * b, 512 * b + 512), R(pn, 0, 512), Fn.Identity, bias=float(512 * b - MID))
+
+    def codev(b):
+        tt(R("Wl", 512 * b, 512 * b + 512), R("q%d" % b, 0, 512), R("s8", 512 * b, 512 * b + 512), Op.add)
+
+    s8(4)
+    pr = prep()
+    next(pr)
+    ts(M("pm", 0), io, C(0), Op.is_equal, C(3), Op.mult)
+    next(pr)
+    ts(M("pm", 1), io, C(5), Op.is_equal, C(3), Op.mult)
+    next(pr)
+    ts(M("pm", 2), io, C(6), Op.is_equal, C(4), Op.mult)
+    ts(M("pm", 3), io, C(0), Op.is_equal, C(4), Op.mult)
+    code("Wh", 4)
+    code("Wl", 4)
+    s8(0)
+    s8(1)
+    code("Wh", 0)
+    code("Wh", 1)
+    s8(2)
+    s8(3)
+    code("Wh", 2)
+    code("Wh", 3)
+    next(pr)
+    codev(0)
+    codev(1)
+    prep2(0)
+    codev(2)
+    codev(3)
+    ts(M("idh"), io, C(0), Op.is_equal, 0.5, Op.mult)
+    ts(M("idk"), io, C(0), Op.is_equal, -K, Op.mult)
+    fill(M("cm", 1), 16.0)
+    fill(M("cm", 2), -1.0 / 128)
+    fill(M("on16"), 1.0 / 16)
+    fill(R("nxb", NP, 208), 0.0)
+    ts(C(7), R("ci", 1, 2), 0.5, Op.add)
+    ts(C(8), R("ci", 1, 2), 16.5, Op.add)
     cp("v", R("thr", 0, 1), R("tac", 0, 1))
 
     starts = [sum(CHUNKS[:k]) for k in range(len(CHUNKS))]
-    nch = len(CHUNKS)
     nloc = 0
 
     for t in range(RO):
         B = S + t * G
 
-        def first(c, wh, q, B=B):
+        def step(name, c, B=B):
             i0, n = starts[c], CHUNKS[c]
-            w = (8 * i0, 8 * (i0 + n))
-            l = (i0 // 2, (i0 + n) // 2)
-            if wh == "l":
-                cp(q, R("L1", *w), I("Wl", 0, TOT + B, "tl1", *l))
-            else:
-                cp(q, R("H1", *w), I("Wh", 0, B, "th1", *l))
-
-        def g1v(c, B=B):
-            i0, n = starts[c], CHUNKS[c]
-            w = (8 * i0, 8 * (i0 + n))
-            l = (i0 // 2, (i0 + n) // 2)
-            tt(R("al", *w), I("Wl", 0, TOT + B, "t2", *l), R("L1", *w), Op.min)
-            tt(R("ah", *w), I("Wh", 0, B, "t2", *l), R("H1", *w), Op.max)
-            scan(R("sl", *w), R("m8n", 0, 8 * n), R("al", *w), 0.0, Op.max, Op.min)
-            cp("v", R("ol", i0, i0 + n), R("sl", 8 * i0 + 7, 8 * (i0 + n), 8))
-            scan(R("sh", *w), R("m8x", 0, 8 * n), R("ah", *w), 0.0, Op.mult, Op.max)
-            tt(R("hc", i0, i0 + n), R("sh", 8 * i0 + 7, 8 * (i0 + n), 8), R("sl", 8 * i0 + 7, 8 * (i0 + n), 8), Op.max)
-            ts(R("oh", i0, i0 + n), R("hc", i0, i0 + n), -4096.0, Op.add)
-
-        def second(c, wh, q, B=B):
-            i0, n = starts[c], CHUNKS[c]
-            if wh == "XL":
-                cp(q, R("XL", 16 * i0, 16 * (i0 + n)), I("X2", 0, UP + B, "ol", i0, i0 + n))
-            else:
-                cp(q, R("XH", 16 * i0, 16 * (i0 + n)), I("X2", UP, UP + B, "oh", i0, i0 + n))
-
-        def blocks(c):
-            i0, n = starts[c], CHUNKS[c]
+            i1 = i0 + n
+            w8, w16, li = (8 * i0, 8 * i1), (16 * i0, 16 * i1), (i0 // 2, i1 // 2)
+            end8, end16 = (8 * i0 + 7, 8 * i1, 8), (16 * i0 + 15, 16 * i1, 16)
             nb = sum((16 * m + 511) // 512 for m in CHUNKS[:c])
-            return [("q%d" % ((nb + k) % 4), 16 * i0 + a, 16 * i0 + min(a + 512, 16 * n)) for k, a in enumerate(range(0, 16 * n, 512))]
+            blocks = [("q%d" % ((nb + k) % 4), 16 * i0 + a, 16 * i0 + min(a + 512, 16 * n)) for k, a in enumerate(range(0, 16 * n, 512))]
+            pd = R("pD" if c % 2 == 0 else "pX", i0, i1)
+            q = "s" if name.islower() else "v"
+            if name in "lL":
+                cp(q, R("L1", *w8), I("Wl", 0, B, "t1", *li))
+            elif name in "hH":
+                cp(q, R("H1", *w8), I("Wh", 0, B, "t1", *li))
+            elif name == "c":
+                act(R("c0", i0, i1), R("L1", 8 * i0, 8 * i1, 8), Fn.Identity, bias=-K)
+            elif name == "A":
+                tt(R("al", *w8), I("Wl", 0, B, "t2", *li), R("L1", *w8), Op.min)
+            elif name == "B":
+                tt(R("ah", *w8), I("Wh", 0, B, "t2", *li), R("H1", *w8), Op.max)
+            elif name == "s":
+                scan(R("sl", *w8), R("m8n", 0, 8 * n), R("al", *w8), 0.0, Op.max, Op.min)
+            elif name == "t":
+                scan(R("sh", *w8), R("m8x", 0, 8 * n), R("ah", *w8), 0.0, Op.min, Op.max)
+            elif name == "p":
+                tt(R("yy", i0, i1), R("sh", *end8), R("c0", i0, i1), Op.max)
+            elif name == "q":
+                tt(R("lo", i0, i1), R("sl", *end8), R("yy", i0, i1), Op.min)
+            elif name == "r":
+                ts(R("ol", i0, i1), R("lo", i0, i1), float(MID), Op.add)
+            elif name == "u":
+                tt(R("hi", i0, i1), R("sh", *end8), R("lo", i0, i1), Op.max)
+            elif name == "v":
+                ts(R("oh", i0, i1), R("hi", i0, i1), float(MID), Op.add)
+            elif name in "xX":
+                cp(q, R("XL", *w16), I("X", 0, B, "ol", i0, i1))
+            elif name in "yY":
+                cp(q, R("XH", *w16), I("X", 0, B, "oh", i0, i1))
+            elif name in "ed":
+                for pn, a, e in blocks:
+                    mm(R(pn, 0, e - a), [(M("idp" if name == "e" else "idn"), R("XL" if name == "e" else "XH", a, e))], name == "e", name == "d")
+            elif name == "b":
+                for pn, a, e in blocks:
+                    act(R("ad", a, e), R(pn, 0, e - a), Fn.Abs)
+            elif name == "D":
+                mm(pd, [(M("om", p), R("ad", 16 * i0 + p, 16 * i1, 16)) for p in range(16)])
+            elif name == "m":
+                scan(R("mxs", *w16), R("m16x", 0, 16 * n), R("XL", *w16), 0.0, Op.min, Op.max)
+            elif name == "n":
+                scan(R("mns", *w16), R("m16n", 0, 16 * n), R("XH", *w16), 0.0, Op.max, Op.min)
+            elif name == "a":
+                mm(R("pU", 256 + i0, 256 + i1), [(M("idh"), R("mxs", *end16)), (M("idh"), R("mns", *end16)),
+                                                 (R("cm", 256, 384, 1, 32), R("ones", 0, n, 1, 32))])
+            elif name == "w":
+                ts(R("nxb", i0, i1), R("pU", 256 + i0, 256 + i1), RND, Op.add, -RND, Op.add)
+            elif name == "f":
+                ts(R("near", i0, i1), pd, R("thr", 0, 1), Op.is_le)
+            elif name == "k":
+                mm(R("pC", i0, i1), [(M("blk"), R("near", i0, i1))])
+            elif name == "g":
+                ts(R("flg", i0, i1), R("pC", i0, i1), 15.5, Op.is_lt)
+            elif name == "j":
+                scan(R("cum", i0, i1), R("ones", i0, i1), R("flg", i0, i1), 0.0 if c == 0 else R("cum", i0 - 1, i0), Op.mult, Op.add)
 
-        def diff(c, part):
-            for pn, a, e in blocks(c):
-                mm(R(pn, 0, e - a), [(R(("idp", "idn")[part], 0, 128), R(("XL", "XH")[part], a, e))], part == 0, part == 1)
-
-        def absd(c):
-            for pn, a, e in blocks(c):
-                act(R("ad", a, e), R(pn, 0, e - a), Fn.Abs)
-
-        def dsum(c):
-            i0, n = starts[c], CHUNKS[c]
-            mm(R("pD" if c % 2 == 0 else "pX", i0, i0 + n), [(R("om", 128 * p, 128 * p + 128), R("ad", 16 * i0 + p, 16 * (i0 + n), 16)) for p in range(16)])
-
-        def farv(c):
-            i0, n = starts[c], CHUNKS[c]
-            ts(R("far", i0, i0 + n), R("pD" if c % 2 == 0 else "pX", i0, i0 + n), R("thr", 0, 1), Op.is_gt)
-
-        def cntp(c):
-            i0, n = starts[c], CHUNKS[c]
-            mm(R("pC", i0, i0 + n), [(R("blk", 0, 128), R("far", i0, i0 + n))])
-
-        def cumv(c):
-            i0, n = starts[c], CHUNKS[c]
-            ts(R("flg", i0, i0 + n), R("pC", i0, i0 + n), 0.0, Op.is_gt)
-            scan(R("cum", i0, i0 + n), R("onesr", i0, i0 + n), R("flg", i0, i0 + n), 0.0 if c == 0 else R("cum", i0 - 1, i0), Op.mult, Op.add)
-
-        def nxv(c):
-            i0, n = starts[c], CHUNKS[c]
-            w = (16 * i0, 16 * (i0 + n))
-            last = (16 * i0 + 15, 16 * (i0 + n), 16)
-            scan(R("mxs", *w), R("m16x", 0, 16 * n), R("XL", *w), 0.0, Op.mult, Op.max)
-            scan(R("mns", *w), R("m16n", 0, 16 * n), R("XH", *w), 0.0, Op.max, Op.min)
-            tt(R("sm", i0, i0 + n), R("mxs", *last), R("mns", *last), Op.add)
-            ts(R("si", i0, i0 + n), R("sm", i0, i0 + n), 0.5, Op.mult, -0.25, Op.add)
-            cp("v", R("nxb", i0, i0 + n), R("si", i0, i0 + n))
-
-        steps = {"l": lambda c: first(c, "l", "s"), "h": lambda c: first(c, "h", "s"), "H": lambda c: first(c, "h", "v"),
-                 "a": g1v, "x": lambda c: second(c, "XL", "s"), "y": lambda c: second(c, "XH", "s"),
-                 "Y": lambda c: second(c, "XH", "v"), "e": lambda c: diff(c, 0), "d": lambda c: diff(c, 1), "b": absd, "D": dsum,
-                 "f": farv, "k": cntp, "c": cumv, "n": nxv}
         for st in ORDER.split():
-            steps[st[0]](int(st[1:]))
+            step(st[0], int(st[1:]))
 
         for h in range(2):
-            act(R("sg", h * NP, h * NP + NP), R("cum", 0, NP), Fn.Sign, bias=R("cf", 2 + h, 3 + h), scale=-1.0, acc=R("cnt2", h, h + 1))
-        if t + 1 < RO:
+            act(R("sg", h * NP, h * NP + NP), R("cum", 0, NP), Fn.Sign, bias=C(7 + h), scale=-1.0, acc=R("cnt2", h, h + 1))
+        more = t + 1 < RO
+        if more:
             prepu(t + 1)
+        mm(R("q0", 0, NP), [(M("id16"), R("io16", 0, NP)), shift(B - MID, NP), (M("idk"), R("near", 0, NP))])
+        if more:
+            ts(R("e8", 0, NP), R("nxb", 0, NP), R("thf", 0, 1), Op.is_lt, K, Op.mult)
+            pr = prep()
+            next(pr)
         ts(R("mo", 0, 2), R("cnt2", 0, 2), 0.5, Op.mult, 96.0, Op.add)
+        if more:
+            next(pr)
         cp("v", R("mailb", t * CAP, (t + 1) * CAP), I("nxb", 0, 208, "mo", 0, 2))
         direct, via = plan[rank, t]
         ml = T.mailb[:, t * CAP:(t + 1) * CAP]
@@ -531,43 +530,31 @@ def rank_program(g, core, T, topo):
                 rid, pid = topo.addr(d, core)
                 ids.append(DstId(rid=rid, pnc=pid))
                 a, b = land(t, f)
-                outs.append(T.X2[:, a:b])
+                outs.append(T.X[:, a:b])
             m, k = emask(topo, core, direct[0][1], False)
             nloc += k
             tr.append(RemoteDMATransfer(dst_ids=ids, dma_engine_mask=m, remote_sem=T.sem["ar%d" % t], srcs=[ml], dsts=outs))
         g.remote_dma_fused(tr, local_sem=T.sem.loc)
 
-        cp("s", R("X2", UP + B, UP + B + NP), R("nxb", 0, NP))
-        if t + 1 < RO:
-            prep(t + 1)
-            kdg()
-            prep2(t + 1)
-            cp("s", R("X2", B, B + NP), R("nxb", 0, NP))
-        mn = R("sl", 7, 1536, 8)
-        ts(R("lq", 0, NP), mn, 4096.0, Op.is_ge, -4096.0, Op.mult)
-        tt(R("lt", 0, NP), mn, R("lq", 0, NP), Op.add)
-        tt(R("fi", 0, NP), R("far", 0, NP), R("iof", B, B + NP), Op.mult)
         j0 = t * G
-        tt(R("An", j0, j0 + NP), R("lt", 0, NP), R("fi", 0, NP), Op.max)
-        dma("y", T.ya[:, j0:j0 + G], T.An[:, j0:j0 + G], [("An", j0, j0 + G)], [])
-        dma("y", T.yx[:, j0:j0 + NP], T.X2[:, UP + B:UP + B + NP], [("X2", UP + B, UP + B + NP)], [])
-
-        def window(a0, a1, names, names4):
-            w = a1 - a0
-            e = a0 - B
-            ts(R("e8", e, e + w), R("X2", UP + a0, UP + a1), R("thf", 0, 1), Op.is_lt, 8192.0, Op.mult)
-            ts(R("e4", e, e + w), R("X2", UP + a0, UP + a1), R("thf", 0, 1), Op.is_lt, 4096.0, Op.mult)
-            tt(R("Wl", a0, a1), names, R("e8", e, e + w), Op.add)
-            tt(R("Wl", TOT + a0, TOT + a1), names, R("e4", e, e + w), Op.add)
-            tt(R("Wh", a0, a1), names4, R("e8", e, e + w), Op.subtract)
-
-        if t + 1 < RO:
-            mm(R("pC", 256, 257), [(R("on16", 0, 128), R("cum", NP - 1, NP))])
+        cp("s", R("X", B, B + NP), R("nxb", 0, NP))
+        if more:
+            next(pr)
+        tt(R("A16", 0, NP), R("q0", 0, NP), R("lo", 0, NP), Op.max)
+        if more:
+            next(pr)
+            mm(R("pC", 256, 257), [(M("on16"), R("cum", NP - 1, NP))])
+            for win, idm, pn in (("Wl", "idp", "q1"), ("Wh", "idn", "q2")):
+                mm(R(pn, 0, NP), [(M("id16"), R("A16", 0, NP)), (M(idm), R("e8", 0, NP))])
+                cp("s", R(win, B, B + NP), R(pn, 0, NP))
             cp("v", R("cci", 0, 1), R("pC", 256, 257))
+            prep2(t + 1)
             ts(R("cci", 1, 2), R("cci", 0, 1), 15, Op.bitwise_and)
+        ts(R("An", j0, j0 + NP), R("A16", 0, NP), float(MID), Op.add)
+        if more:
             tt(R("thr", 0, 1), R("cci", 1, 2), R("tac", 0, 1), Op.add)
-            ts(R("a4", 0, NP), R("An", j0, j0 + NP), 4096.0, Op.add)
-            window(B, B + NP, R("An", j0, j0 + NP), R("a4", 0, NP))
+        dma("y", T.yx[:, j0:j0 + NP], T.X[:, B:B + NP], [("X", B, B + NP)], [])
+        dma("y", T.ya[:, j0:j0 + G], T.An[:, j0:j0 + G], [("An", j0, j0 + G)], [])
 
         key = "ar%d" % t
         narr = 0
@@ -578,11 +565,13 @@ def rank_program(g, core, T, topo):
             narr += emask(topo, s, core, False)[1]
         semof[key] = T.sem[key]
         clock[key, narr] = {}
-        note(key, narr, [], [("X2", UP + B + NP, UP + B + G)])
-        if t + 1 < RO:
-            window(B + NP, B + G, R("iof", B + NP, B + G), R("iof4", j0 + NP, j0 + G))
-            cp("s", R("X2", B + NP, B + G), R("X2", UP + B + NP, UP + B + G))
-        dma("y", T.yx[:, j0 + NP:j0 + G], T.X2[:, UP + B + NP:UP + B + G], [("X2", UP + B + NP, UP + B + G)], [])
+        note(key, narr, [], [("X", B + NP, B + G)])
+        if more:
+            names = R("iom", t * FO * CAP, (t + 1) * FO * CAP)
+            ts(R("e8", NP, G), R("X", B + NP, B + G), R("thf", 0, 1), Op.is_lt, K, Op.mult)
+            tt(R("Wl", B + NP, B + G), names, R("e8", NP, G), Op.add)
+            tt(R("Wh", B + NP, B + G), names, R("e8", NP, G), Op.subtract)
+        dma("y", T.yx[:, j0 + NP:j0 + G], T.X[:, B + NP:B + G], [("X", B + NP, B + G)], [])
 
     g.wait_ge(T.sem.loc, nloc)
     for q in ("v", "s", "p", "g"):

@@ -7,9 +7,10 @@ TOT = S + RO * G
 K = 8192.0
 MID = 2048
 RND = 12582912.0
-CHUNKS = [64, 64, 64]
-ORDER = ("l0 H0 c0 l1 A0 B0 h1 s0 t0 c1 p0 q0 r0 l2 u0 v0 x0 A1 B1 c2 y0 e0 s1 t1 d0 p1 q1 r1 u1 v1 H2 A2 B2 x1 b0 s2 t2 p2 q2 r2 u2 v2 "
-         "y1 e1 D0 m0 n0 d1 x2 Y2 a0 b1 e2 m1 n1 d2 w0 a1 D1 b2 m2 w1 n2 f0 f1 a2 D2 k0 k1 w2 g0 g1 f2 k2 j0 j1 g2 j2")
+UNIT = 32
+ORDER = ("H01 l01 B01 h23 A01 l23 t01 c01 l45 s01 p01 B23 c23 h45 q01 t23 r01 A23 x01 p23 u01 s23 v01 C45 q23 B45 y01 e01 r23 A45 "
+         "t45 x23 d01 s45 p45 u23 q45 v23 u45 r45 Y23 b01 e23 v45 X45 D01 y45 d23 m01 e45 b23 n01 d45 n23 D23 b45 m45 n45 f03 m23 "
+         "k03 D45 g03 a03 f45 j03 k45 z03 g45 w03 j45 a45 z45 Z0 w45")
 
 SCRATCH = {
     "X": ("sbuf", [128, TOT], "bfloat16"),
@@ -19,9 +20,10 @@ SCRATCH = {
     "k16": ("sbuf", [128, 256], "float16"),
     "ksel": ("sbuf", [128, 1024], "bfloat16"),
     "kdt": ("sbuf", [128, U], "float32"),
-    "ones": ("sbuf", [128, 1024], "bfloat16"),
+    "ones": ("sbuf", [128, 512], "bfloat16"),
     "io16": ("sbuf", [128, 512], "float16"),
-    "ib": ("sbuf", [128, 128], "bfloat16"),
+    "ib": ("sbuf", [128, 384], "bfloat16"),
+    "pj": ("sbuf", [128, 32], "float32"),
     "cm": ("sbuf", [128, 384], "bfloat16"),
     "s8": ("sbuf", [128, S], "bfloat16"),
     "An": ("sbuf", [128, RO * G], "float32"),
@@ -41,9 +43,7 @@ SCRATCH = {
     "idn": ("sbuf", [128, 128], "bfloat16"),
     "idh": ("sbuf", [128, 128], "bfloat16"),
     "idk": ("sbuf", [128, 128], "bfloat16"),
-    "on16": ("sbuf", [128, 128], "bfloat16"),
-    "id16": ("sbuf", [128, 128], "float16"),
-    "pm": ("sbuf", [128, 512], "float16"),
+    "pm": ("sbuf", [128, 512], "bfloat16"),
     "om": ("sbuf", [128, 2048], "bfloat16"),
     "wm": ("sbuf", [128, 2048], "bfloat16"),
     "m8x": ("sbuf", [128, 512], "bfloat16"),
@@ -78,16 +78,13 @@ SCRATCH = {
     "flg": ("sbuf", [128, NP], "bfloat16"),
     "cum": ("sbuf", [128, NP], "bfloat16"),
     "sg": ("sbuf", [128, 2 * NP], "bfloat16"),
-    "cnt2": ("sbuf", [128, 2], "float32"),
+    "cnt2": ("sbuf", [128, 6], "float32"),
     "mo": ("sbuf", [128, 2], "uint16"),
     "mailb": ("sbuf", [128, RO * CAP], "bfloat16"),
     "rbuf": ("sbuf", [128, RO * CAP], "bfloat16"),
     "A16": ("sbuf", [128, NP], "float16"),
     "e8": ("sbuf", [128, G], "bfloat16"),
-    "q0": ("psum", [128, 512], "float32"),
-    "q1": ("psum", [128, 512], "float32"),
-    "q2": ("psum", [128, 512], "float32"),
-    "q3": ("psum", [128, 512], "float32"),
+    "pq": ("psum", [128, 2048], "float32"),
     "pD": ("psum", [128, 512], "float32"),
     "pX": ("psum", [128, 512], "float32"),
     "pC": ("psum", [128, 512], "float32"),
@@ -220,7 +217,11 @@ def rank_program(g, core, T, topo):
         note(key, 16, reads, writes)
 
     def R(name, a, b, step=1, rows=128):
-        return (T[name][0:rows, a:b:step] if step != 1 else T[name][0:rows, a:b], [(name, a, b)])
+        regs = [("q%d" % k, a, b) for k in range(a // 512, (b + 511) // 512)] if name == "pq" else [(name, a, b)]
+        return (T[name][0:rows, a:b:step] if step != 1 else T[name][0:rows, a:b], regs)
+
+    def Q(k, a, b):
+        return R("pq", 512 * k + a, 512 * k + b)
 
     def I(win, a, b, off, c, d):
         return (T[win][:, a:b].indirect(T[off][:, c:d]), [(win, a, b), (off, c, d)])
@@ -238,6 +239,9 @@ def rank_program(g, core, T, topo):
         if isinstance(bias, tuple):
             rd += bias[1]
             bb = bias[0]
+        if isinstance(scale, tuple):
+            rd += scale[1]
+            scale = scale[0]
         if acc is not None:
             wr += acc[1]
             op("s", [lambda: g.scalar.activation(out[0], in_[0], func, bias=bb, scale=scale, accum_out=acc[0])], rd, wr)
@@ -302,39 +306,45 @@ def rank_program(g, core, T, topo):
     dma("s", T.X[:, 2048:S], T.x0[:, 2048:S], [], [("X", 2048, S)])
     dma("y", T.kq[:], T.kd[:], [], [("kq", 0, 256)])
     dma("s", T.thc[:], T.th[:], [], [("thc", 0, 1)])
-    dma("y", T.X[:, 0:1024], T.x0[:, 0:1024], [], [("X", 0, 1024)])
-    dma("s", T.X[:, 1024:2048], T.x0[:, 1024:2048], [], [("X", 1024, 2048)])
+    dma("s", T.X[:, 0:1024], T.x0[:, 0:1024], [], [("X", 0, 1024)])
+    dma("y", T.X[:, 1024:2048], T.x0[:, 1024:2048], [], [("X", 1024, 2048)])
     dma("y", T.tac[:], T.tau[:], [], [("tac", 0, 1)])
 
-    fill(R("ones", 0, 1024), 1.0)
     iota(R("ci", 0, 1), [[0, 1]], 0, 1, False)
-    iota(R("ib", 0, 128), [[1, 8], [0, 16]], 0, 0)
-    asel(R("ksel", 0, 1024), R("ones", 0, 1024), [[-1, 8], [0, 8], [-8, 16]], Op.is_equal, 0, 1)
+    iota(R("pj", 0, 9), [[-1, 9]], 0, 1)
+    iota(M("ib", 0), [[1, 8], [8, 16]], 0, 0)
+    iota(R("pj", 16, 32), [[8, 16]], 0, 0)
+    iota(M("ib", 1), [[0, 8], [8, 16]], 0, 0)
+    iota(M("ib", 2), [[1, 8], [0, 16]], 0, 0)
     iota(R("k613", 0, 12), [[613 * 16, 12]], 0, 0)
-    fill(R("wm", 0, 2048), 0.0)
-    scan(R("io16", 0, 512), R("ones", 0, 512), R("ones", 0, 512), -1.0, Op.mult, Op.add)
-    ts(R("ci", 1, 2), R("ci", 0, 1), 15, Op.bitwise_and)
+    fill(R("ones", 0, 512), 1.0)
     ts(R("ci", 2, 3), R("ci", 0, 1), 4, Op.arith_shift_right)
-    cp("v", C(0), R("ci", 0, 1))
-    fill(M("cm", 0), -16.0)
+    ts(R("ci", 1, 2), R("ci", 0, 1), 15, Op.bitwise_and)
+    scan(R("io16", 0, 512), R("ones", 0, 512), R("ones", 0, 512), -1.0, Op.mult, Op.add)
     cp("v", C(1), R("ci", 2, 3))
-    ts(C(2), R("ci", 1, 2), 613.0, Op.mult)
-    io = R("io16", 0, 128)
-    ts(M("id16"), io, C(0), Op.is_equal)
-    ts(M("blk"), M("ib"), C(1), Op.is_equal)
-    ts(M("idn"), io, C(0), Op.is_equal, -1.0, Op.mult)
-    ts(M("idp"), io, C(0), Op.is_equal)
+    for j, v in enumerate((-16.0, 16.0, -1.0 / 128)):
+        act(M("cm", j), M("ones"), Fn.Copy, scale=v)
+    act(R("nxb", NP, 208), R("ones", 0, 16), Fn.Copy, scale=0.0)
+    io, row = R("io16", 0, 128), R("pj", 0, 1)
+    ts(M("idp"), io, row, Op.is_equal)
+    ts(R("pj", 16, 32), R("pj", 16, 32), C(1), Op.add)
+    ts(C(3), R("ci", 1, 2), 8, Op.is_lt)
+    ts(C(4), R("ci", 1, 2), 8, Op.is_ge)
+    ts(C(5), row, 8.0, Op.add)
+    for nm, v in (("idn", -1.0), ("idh", 0.5), ("idk", -K)):
+        act(M(nm), M("idp"), Fn.Copy, scale=v)
+    act(M("pm", 0), M("idp"), Fn.Copy, scale=C(3))
+    act(M("pm", 3), M("idp"), Fn.Copy, scale=C(4))
     for b in range(4):
-        mm(R("q%d" % b, 0, 512), [(M("id16"), R("io16", 0, 512)), shift(512 * b - MID, 512)])
+        mm(Q(b, 0, 512), [(M("idp"), R("io16", 0, 512)), shift(512 * b - MID, 512)])
+    for j in range(16):
+        ts(M("om", j), M("ib", 0), R("pj", 16 + j, 17 + j), Op.is_equal)
+    for j in range(8):
+        ts(M("ksel", j), M("ib", 1), R("pj", j, j + 1), Op.is_equal)
+    cp("v", R("thf", 0, 1), R("thc", 0, 1))
     cp("v", R("wtf", 0, 1), R("wtc", 0, 1))
-    ts(R("k16", 0, 256), R("kq", 0, 256), -2048.0, Op.add)
-    for a in range(8):
-        ts(R("wm", 16 * a, 16 * a + 129 * 15 + 1, 129), R("blk", 16 * a, 16 * a + 16), R("wtf", 0, 1), Op.mult)
     iota(R("m8n", 0, 512), [[0, 64], [-20480, 8]], 16384, 0)
     iota(R("m8x", 0, 512), [[0, 64], [20480, 8]], -16384, 0)
-    iota(R("om", 0, 2048), [[0, 2048]], 0, 0)
-    for a in range(8):
-        asel(R("om", 16 * a, 16 * a + 129 * 15 + 1, 129), R("blk", 16 * a, 16 * a + 16), [[0, 16]], Op.is_ge, 0, 0)
     iota(R("m16x", 0, 1024), [[0, 64], [256, 16]], 0, 0)
     iota(R("m16n", 0, 1024), [[0, 64], [-256, 16]], 256, 0)
     iota(R("iom", 0, RO * FO * CAP), [[G, RO], [1, FO * CAP]], S + NP - MID, 0)
@@ -363,82 +373,87 @@ def rank_program(g, core, T, topo):
         ts(R("t2", 0, 96), R("pU", 96, 192), sc, Op.mult, off, Op.add)
 
     rot = ["pD", "pX", "pC"]
-    for b in range(4):
+    nrot = [0]
+
+    def bank():
+        nrot[0] += 1
+        return rot[nrot[0] % 3]
+
+    def spread(b, q):
+        pn = bank()
         for h in range(2):
-            mm(R(rot[b % 3], 256 * h, 256 * h + 256), [(M("ksel", 2 * b + h), R("k16", 0, 256))])
-        if b == 1:
-            prepu(0)
-        cp("s" if b != 1 else "v", R("kdt", 512 * b, 512 * b + 512), R(rot[b % 3], 0, 512))
-    cp("v", R("thf", 0, 1), R("thc", 0, 1))
-    ts(R("k613", 0, 12), R("k613", 0, 12), C(2), Op.add)
-    ts(C(3), R("ci", 1, 2), 8, Op.is_lt)
-    ts(C(4), R("ci", 1, 2), 8, Op.is_ge)
-    ts(C(5), C(0), 8.0, Op.add)
-    ts(C(6), C(0), -8.0, Op.add)
+            mm(R(pn, 256 * h, 256 * h + 256), [(M("ksel", 2 * b + h), R("k16", 0, 256))])
+        cp(q, R("kdt", 512 * b, 512 * b + 512), R(pn, 0, 512))
 
     def s8(b):
         ts(R("s8", 512 * b, 512 * b + 512), R("X", 512 * b, 512 * b + 512), R("thf", 0, 1), Op.is_lt, K, Op.mult)
 
-    nrot = [1]
-
     def code(win, b):
-        pn = rot[nrot[0] % 3]
-        nrot[0] += 1
-        mm(R(pn, 0, 512), [(M("id16"), R("io16", 0, 512)), (M("idp" if win == "Wl" else "idn"), R("s8", 512 * b, 512 * b + 512))])
+        pn = bank()
+        mm(R(pn, 0, 512), [(M("idp"), R("io16", 0, 512)), (M("idp" if win == "Wl" else "idn"), R("s8", 512 * b, 512 * b + 512))])
         act(R(win, 512 * b, 512 * b + 512), R(pn, 0, 512), Fn.Identity, bias=float(512 * b - MID))
 
     def codev(b):
-        tt(R("Wl", 512 * b, 512 * b + 512), R("q%d" % b, 0, 512), R("s8", 512 * b, 512 * b + 512), Op.add)
+        tt(R("Wl", 512 * b, 512 * b + 512), Q(b, 0, 512), R("s8", 512 * b, 512 * b + 512), Op.add)
 
     s8(4)
+    code("Wl", 4)
+    code("Wh", 4)
+    ts(C(2), R("ci", 1, 2), 613.0, Op.mult)
+    ts(R("k16", 0, 256), R("kq", 0, 256), -2048.0, Op.add)
+    ts(R("wm", 0, 2048), R("om", 0, 2048), R("wtf", 0, 1), Op.mult)
+    spread(0, "s")
+    s8(0)
+    s8(1)
+    spread(1, "v")
+    spread(2, "s")
+    prepu(0)
+    spread(3, "s")
+    ts(R("k613", 0, 12), R("k613", 0, 12), C(2), Op.add)
+    code("Wh", 0)
+    code("Wh", 1)
     pr = prep()
-    next(pr)
-    ts(M("pm", 0), io, C(0), Op.is_equal, C(3), Op.mult)
     next(pr)
     ts(M("pm", 1), io, C(5), Op.is_equal, C(3), Op.mult)
     next(pr)
-    ts(M("pm", 2), io, C(6), Op.is_equal, C(4), Op.mult)
-    ts(M("pm", 3), io, C(0), Op.is_equal, C(4), Op.mult)
-    code("Wh", 4)
-    code("Wl", 4)
-    s8(0)
-    s8(1)
-    code("Wh", 0)
-    code("Wh", 1)
+    ts(M("pm", 2), io, R("pj", 8, 9), Op.is_equal, C(4), Op.mult)
+    next(pr)
     s8(2)
     s8(3)
+    next(pr)
     code("Wh", 2)
     code("Wh", 3)
-    next(pr)
     codev(0)
     codev(1)
     prep2(0)
     codev(2)
     codev(3)
-    ts(M("idh"), io, C(0), Op.is_equal, 0.5, Op.mult)
-    ts(M("idk"), io, C(0), Op.is_equal, -K, Op.mult)
-    fill(M("cm", 1), 16.0)
-    fill(M("cm", 2), -1.0 / 128)
-    fill(M("on16"), 1.0 / 16)
-    fill(R("nxb", NP, 208), 0.0)
-    ts(C(7), R("ci", 1, 2), 0.5, Op.add)
-    ts(C(8), R("ci", 1, 2), 16.5, Op.add)
-    cp("v", R("thr", 0, 1), R("tac", 0, 1))
 
-    starts = [sum(CHUNKS[:k]) for k in range(len(CHUNKS))]
+    def later():
+        ts(M("blk"), M("ib", 2), C(1), Op.is_equal)
+        yield
+        ts(C(7), R("ci", 1, 2), 0.5, Op.add)
+        yield
+        ts(C(8), R("ci", 1, 2), 16.5, Op.add)
+        yield
+        cp("v", R("thr", 0, 1), R("tac", 0, 1))
+        while True:
+            yield
+
+    late = later()
     nloc = 0
 
     for t in range(RO):
         B = S + t * G
 
-        def step(name, c, B=B):
-            i0, n = starts[c], CHUNKS[c]
-            i1 = i0 + n
+        def step(name, c, c1, B=B):
+            i0, i1 = UNIT * c, UNIT * (c1 + 1)
+            n = i1 - i0
             w8, w16, li = (8 * i0, 8 * i1), (16 * i0, 16 * i1), (i0 // 2, i1 // 2)
             end8, end16 = (8 * i0 + 7, 8 * i1, 8), (16 * i0 + 15, 16 * i1, 16)
-            nb = sum((16 * m + 511) // 512 for m in CHUNKS[:c])
-            blocks = [("q%d" % ((nb + k) % 4), 16 * i0 + a, 16 * i0 + min(a + 512, 16 * n)) for k, a in enumerate(range(0, 16 * n, 512))]
-            pd = R("pD" if c % 2 == 0 else "pX", i0, i1)
+            nb = c % 4
+            blocks = [(nb + k, 16 * i0 + a, 16 * i0 + min(a + 512, 16 * n)) for k, a in enumerate(range(0, 16 * n, 512))]
+            pd = R("pD" if i1 < NP else "pX", i0, i1)
             q = "s" if name.islower() else "v"
             if name in "lL":
                 cp(q, R("L1", *w8), I("Wl", 0, B, "t1", *li))
@@ -446,6 +461,8 @@ def rank_program(g, core, T, topo):
                 cp(q, R("H1", *w8), I("Wh", 0, B, "t1", *li))
             elif name == "c":
                 act(R("c0", i0, i1), R("L1", 8 * i0, 8 * i1, 8), Fn.Identity, bias=-K)
+            elif name == "C":
+                ts(R("c0", i0, i1), R("L1", 8 * i0, 8 * i1, 8), -K, Op.add)
             elif name == "A":
                 tt(R("al", *w8), I("Wl", 0, B, "t2", *li), R("L1", *w8), Op.min)
             elif name == "B":
@@ -470,10 +487,9 @@ def rank_program(g, core, T, topo):
                 cp(q, R("XH", *w16), I("X", 0, B, "oh", i0, i1))
             elif name in "ed":
                 for pn, a, e in blocks:
-                    mm(R(pn, 0, e - a), [(M("idp" if name == "e" else "idn"), R("XL" if name == "e" else "XH", a, e))], name == "e", name == "d")
+                    mm(Q(pn, 0, e - a), [(M("idp" if name == "e" else "idn"), R("XL" if name == "e" else "XH", a, e))], name == "e", name == "d")
             elif name == "b":
-                for pn, a, e in blocks:
-                    act(R("ad", a, e), R(pn, 0, e - a), Fn.Abs)
+                act(R("ad", *w16), Q(nb, 0, 16 * n), Fn.Abs)
             elif name == "D":
                 mm(pd, [(M("om", p), R("ad", 16 * i0 + p, 16 * i1, 16)) for p in range(16)])
             elif name == "m":
@@ -493,21 +509,28 @@ def rank_program(g, core, T, topo):
                 ts(R("flg", i0, i1), R("pC", i0, i1), 15.5, Op.is_lt)
             elif name == "j":
                 scan(R("cum", i0, i1), R("ones", i0, i1), R("flg", i0, i1), 0.0 if c == 0 else R("cum", i0 - 1, i0), Op.mult, Op.add)
+            elif name == "z":
+                for h in range(2):
+                    k = h + (2 if c else 0)
+                    act(R("sg", h * NP + i0, h * NP + i1), R("cum", i0, i1), Fn.Sign, bias=C(7 + h), scale=-1.0, acc=R("cnt2", k, k + 1))
+            elif name == "Z":
+                ts(R("cnt2", 4, 6), R("cnt2", 0, 2), float(NP), Op.add)
+            if name in "pqu":
+                next(late)
 
         for st in ORDER.split():
-            step(st[0], int(st[1:]))
+            step(st[0], int(st[1]), int(st[-1]))
 
-        for h in range(2):
-            act(R("sg", h * NP, h * NP + NP), R("cum", 0, NP), Fn.Sign, bias=C(7 + h), scale=-1.0, acc=R("cnt2", h, h + 1))
         more = t + 1 < RO
         if more:
             prepu(t + 1)
-        mm(R("q0", 0, NP), [(M("id16"), R("io16", 0, NP)), shift(B - MID, NP), (M("idk"), R("near", 0, NP))])
+        mm(Q(0, 0, NP), [(M("idp"), R("io16", 0, NP)), shift(B - MID, NP), (M("idk"), R("near", 0, NP))])
         if more:
             ts(R("e8", 0, NP), R("nxb", 0, NP), R("thf", 0, 1), Op.is_lt, K, Op.mult)
             pr = prep()
             next(pr)
-        ts(R("mo", 0, 2), R("cnt2", 0, 2), 0.5, Op.mult, 96.0, Op.add)
+        for h in range(2):
+            ts(R("mo", h, h + 1), R("cnt2", 2 + h, 3 + h), R("cnt2", 4 + h, 5 + h), Op.add, 0.5, Op.mult)
         if more:
             next(pr)
         cp("v", R("mailb", t * CAP, (t + 1) * CAP), I("nxb", 0, 208, "mo", 0, 2))
@@ -540,16 +563,16 @@ def rank_program(g, core, T, topo):
         cp("s", R("X", B, B + NP), R("nxb", 0, NP))
         if more:
             next(pr)
-        tt(R("A16", 0, NP), R("q0", 0, NP), R("lo", 0, NP), Op.max)
+        tt(R("A16", 0, NP), Q(0, 0, NP), R("lo", 0, NP), Op.max)
         if more:
             next(pr)
-            mm(R("pC", 256, 257), [(M("on16"), R("cum", NP - 1, NP))])
-            for win, idm, pn in (("Wl", "idp", "q1"), ("Wh", "idn", "q2")):
-                mm(R(pn, 0, NP), [(M("id16"), R("A16", 0, NP)), (M(idm), R("e8", 0, NP))])
-                cp("s", R(win, B, B + NP), R(pn, 0, NP))
+            mm(R("pC", 256, 257), [(M("ones"), R("cum", NP - 1, NP))])
+            for win, idm, pn in (("Wl", "idp", 1), ("Wh", "idn", 2)):
+                mm(Q(pn, 0, NP), [(M("idp"), R("A16", 0, NP)), (M(idm), R("e8", 0, NP))])
+                cp("s", R(win, B, B + NP), Q(pn, 0, NP))
             cp("v", R("cci", 0, 1), R("pC", 256, 257))
             prep2(t + 1)
-            ts(R("cci", 1, 2), R("cci", 0, 1), 15, Op.bitwise_and)
+            ts(R("cci", 1, 2), R("cci", 0, 1), 4, Op.arith_shift_right, 15, Op.bitwise_and)
         ts(R("An", j0, j0 + NP), R("A16", 0, NP), float(MID), Op.add)
         if more:
             tt(R("thr", 0, 1), R("cci", 1, 2), R("tac", 0, 1), Op.add)

from concourse.bass import DstId, RemoteDMATransfer
from concourse.mybir import AluOpType as Op, ActivationFunctionType as Fn

S, U, NP, CAP, FO, RO = 2560, 2048, 192, 32, 2, 4
G = NP + FO * CAP
TOT = S + RO * G
K = 8192.0
MID = 2048
RND = 12582912.0
UNIT = 32
ORDER = ("H01 l01 B01 h23 A01 l23 t01 c01 l45 s01 p01 B23 c23 h45 q01 t23 r01 A23 x01 p23 u01 s23 v01 C45 q23 B45 y01 e01 r23 A45 "
         "t45 x23 d01 s45 p45 u23 q45 v23 u45 r45 Y23 b01 e23 v45 X45 D01 y45 d23 m01 e45 b23 n01 d45 n23 D23 b45 m45 n45 f03 m23 "
         "k03 D45 g03 a03 f45 j03 k45 z03 g45 w03 j45 a45 z45 Z0 w45")

SCRATCH = {
    "X": ("sbuf", [128, TOT], "bfloat16"),
    "Wl": ("sbuf", [128, TOT], "float32"),
    "Wh": ("sbuf", [128, TOT], "float32"),
    "kq": ("sbuf", [128, 256], "int32"),
    "k16": ("sbuf", [128, 256], "float16"),
    "ksel": ("sbuf", [128, 1024], "bfloat16"),
    "kdt": ("sbuf", [128, U], "float32"),
    "ones": ("sbuf", [128, 512], "bfloat16"),
    "io16": ("sbuf", [128, 512], "float16"),
    "ib": ("sbuf", [128, 384], "bfloat16"),
    "pj": ("sbuf", [128, 32], "float32"),
    "cm": ("sbuf", [128, 384], "bfloat16"),
    "s8": ("sbuf", [128, S], "bfloat16"),
    "An": ("sbuf", [128, RO * G], "float32"),
    "iom": ("sbuf", [128, RO * FO * CAP], "float32"),
    "ci": ("sbuf", [128, 16], "int32"),
    "cf": ("sbuf", [128, 16], "float32"),
    "k613": ("sbuf", [128, 12], "float32"),
    "wtc": ("sbuf", [128, 1], "int32"),
    "thc": ("sbuf", [128, 1], "int32"),
    "tac": ("sbuf", [128, 1], "int32"),
    "wtf": ("sbuf", [128, 1], "float32"),
    "thf": ("sbuf", [128, 1], "float32"),
    "thr": ("sbuf", [128, 1], "float32"),
    "cci": ("sbuf", [128, 2], "int32"),
    "blk": ("sbuf", [128, 128], "bfloat16"),
    "idp": ("sbuf", [128, 128], "bfloat16"),
    "idn": ("sbuf", [128, 128], "bfloat16"),
    "idh": ("sbuf", [128, 128], "bfloat16"),
    "idk": ("sbuf", [128, 128], "bfloat16"),
    "pm": ("sbuf", [128, 512], "bfloat16"),
    "om": ("sbuf", [128, 2048], "bfloat16"),
    "wm": ("sbuf", [128, 2048], "bfloat16"),
    "m8x": ("sbuf", [128, 512], "bfloat16"),
    "m8n": ("sbuf", [128, 512], "bfloat16"),
    "m16x": ("sbuf", [128, 1024], "bfloat16"),
    "m16n": ("sbuf", [128, 1024], "bfloat16"),
    "ui": ("sbuf", [128, 12], "int32"),
    "um": ("sbuf", [128, 12], "int32"),
    "uo": ("sbuf", [128, 12], "uint16"),
    "ke": ("sbuf", [128, NP], "float16"),
    "t1": ("sbuf", [128, 96], "uint16"),
    "t2": ("sbuf", [128, 96], "uint16"),
    "L1": ("sbuf", [128, 1536], "float32"),
    "H1": ("sbuf", [128, 1536], "float32"),
    "al": ("sbuf", [128, 1536], "float16"),
    "ah": ("sbuf", [128, 1536], "float16"),
    "sl": ("sbuf", [128, 1536], "float16"),
    "sh": ("sbuf", [128, 1536], "float16"),
    "c0": ("sbuf", [128, NP], "float32"),
    "yy": ("sbuf", [128, NP], "float16"),
    "lo": ("sbuf", [128, NP], "float16"),
    "hi": ("sbuf", [128, NP], "float16"),
    "ol": ("sbuf", [128, NP], "uint16"),
    "oh": ("sbuf", [128, NP], "uint16"),
    "XL": ("sbuf", [128, 3072], "bfloat16"),
    "XH": ("sbuf", [128, 3072], "bfloat16"),
    "ad": ("sbuf", [128, 3072], "bfloat16"),
    "mxs": ("sbuf", [128, 3072], "bfloat16"),
    "mns": ("sbuf", [128, 3072], "bfloat16"),
    "nxb": ("sbuf", [128, 208], "bfloat16"),
    "near": ("sbuf", [128, NP], "bfloat16"),
    "flg": ("sbuf", [128, NP], "bfloat16"),
    "cum": ("sbuf", [128, NP], "bfloat16"),
    "sg": ("sbuf", [128, 2 * NP], "bfloat16"),
    "cnt2": ("sbuf", [128, 6], "float32"),
    "mo": ("sbuf", [128, 2], "uint16"),
    "mailb": ("sbuf", [128, RO * CAP], "bfloat16"),
    "rbuf": ("sbuf", [128, RO * CAP], "bfloat16"),
    "A16": ("sbuf", [128, NP], "float16"),
    "e8": ("sbuf", [128, G], "bfloat16"),
    "pq": ("psum", [128, 2048], "float32"),
    "pD": ("psum", [128, 512], "float32"),
    "pX": ("psum", [128, 512], "float32"),
    "pC": ("psum", [128, 512], "float32"),
    "pU": ("psum", [128, 512], "float32"),
}
PSUM = ("q0", "q1", "q2", "q3", "pD", "pX", "pC", "pU")
NDMA = 24
SEMAPHORES = (["sv", "ss", "sp", "sg", "loc"] + ["ar%d" % t for t in range(RO)] + ["rl%d" % t for t in range(RO)]
              + ["d%d" % i for i in range(NDMA)])


def routes(T, topo):
    n = len(T.cores)
    relay = {}
    plan = {}
    for r in range(n):
        src = T.cores[r]
        far = [d for d in T.cores if d != src and not topo.may_write(src, d)]
        relay[r] = [c for c in topo.cores_of(src) if c not in T.cores and topo.die(c) == topo.die(src)
                    and all(topo.may_write(c, d) for d in far)][:2]
        for t in range(RO):
            ds = [T.cores[(r + 1 + ((FO * t + f) % (n - 1))) % n] for f in range(FO)]
            plan[r, t] = ([(f, d) for f, d in enumerate(ds) if topo.may_write(src, d)],
                          [(f, d) for f, d in enumerate(ds) if not topo.may_write(src, d)])
    return relay, plan


def emask(topo, src, dst, high, full=False):
    es = topo.engines(src, dst)
    if not full:
        es = es[8:16] if high else es[:8]
    return sum(1 << e for e in es), len(es)


def land(t, f):
    b = S + t * G + NP + f * CAP
    return b, b + CAP


def relay_program(g, core, T, topo, r, which, plan):
    sent = 0
    for t in range(RO):
        ds = plan[r, t][1][which:which + 1]
        if not ds:
            continue
        n = emask(topo, T.cores[r], core, True, not plan[r, t][0])[1]
        g.wait_ge(T.sem["rl%d" % t], n)
        m, k = emask(topo, core, ds[0][1], False)
        ids, outs = [], []
        for f, d in ds:
            rid, pid = topo.addr(d, core)
            ids.append(DstId(rid=rid, pnc=pid))
            a, b = land(t, f)
            outs.append(T.X[:, a:b])
        g.remote_dma_fused([RemoteDMATransfer(dst_ids=ids, dma_engine_mask=m, remote_sem=T.sem["ar%d" % t],
                                              srcs=[T.rbuf[:, t * CAP:(t + 1) * CAP]], dsts=outs)], local_sem=T.sem.loc)
        sent += k
    if sent:
        g.wait_ge(T.sem.loc, sent)


def rank_program(g, core, T, topo):
    relay, plan = routes(T, topo)
    rank = T.rank_of(core)
    if rank is None:
        for r in relay:
            if core in relay[r]:
                relay_program(g, core, T, topo, r, relay[r].index(core), plan)
        return

    queue = {"v": g.vector, "s": g.scalar, "p": g.tensor, "g": g, "y": g.sync}
    semof = {"v": T.sem.sv, "s": T.sem.ss, "p": T.sem.sp, "g": T.sem.sg}
    count = {"v": 0, "s": 0, "p": 0, "g": 0}
    known = {q: {} for q in queue}
    clock = {}
    hist = {}
    ndma = [0]

    def need(q, reads, writes):
        want = {}
        for kind, regs in (("r", reads), ("w", writes)):
            for name, a, b in regs:
                ps = name in PSUM
                for (hk, ha, hb, hq, hi) in hist.get(name, ()):
                    if ps:
                        if hq == q and hk == "r":
                            continue
                        if hq == q and (hb <= a or b <= ha):
                            continue
                    else:
                        if hb <= a or b <= ha or (hk == "r" and kind == "r"):
                            continue
                        if hq == q and hk == "r":
                            continue
                    if want.get(hq, 0) < hi:
                        want[hq] = hi
        return want

    def dowait(q, want):
        for hq in sorted(want, key=lambda k: (k == q, k)):
            hi = want[hq]
            if known[q].get(hq, 0) >= hi:
                continue
            queue[q].wait_ge(semof[hq], hi)
            for k2, v2 in clock[hq, hi].items():
                if known[q].get(k2, 0) < v2:
                    known[q][k2] = v2
            known[q][hq] = hi

    def note(q, hi, reads, writes):
        for kind, regs in (("r", reads), ("w", writes)):
            for name, a, b in regs:
                hist.setdefault(name, []).append((kind, a, b, q, hi))

    def op(q, fns, reads, writes, goes_on=False):
        dowait(q, need(q, reads, [] if goes_on else writes))
        for fn in fns:
            fn().then_inc(semof[q], 1)
            count[q] += 1
            clock[q, count[q]] = dict(known[q])
        note(q, count[q], reads, writes)

    def dma(q, out, in_, reads, writes):
        dowait(q, need(q, reads, writes))
        key = "d%d" % ndma[0]
        ndma[0] += 1
        semof[key] = T.sem[key]
        queue[q].dma_start(out, in_).then_inc(T.sem[key], 16)
        clock[key, 16] = dict(known[q])
        note(key, 16, reads, writes)

    def R(name, a, b, step=1, rows=128):
        regs = [("q%d" % k, a, b) for k in range(a // 512, (b + 511) // 512)] if name == "pq" else [(name, a, b)]
        return (T[name][0:rows, a:b:step] if step != 1 else T[name][0:rows, a:b], regs)

    def Q(k, a, b):
        return R("pq", 512 * k + a, 512 * k + b)

    def I(win, a, b, off, c, d):
        return (T[win][:, a:b].indirect(T[off][:, c:d]), [(win, a, b), (off, c, d)])

    def cp(q, out, in_):
        if q == "v":
            op("v", [lambda: g.vector.tensor_copy(out[0], in_[0])], in_[1], out[1])
        else:
            op("s", [lambda: g.scalar.activation(out[0], in_[0], Fn.Copy)], in_[1], out[1])

    def act(out, in_, func, bias=0.0, scale=1.0, acc=None):
        rd = list(in_[1])
        wr = list(out[1])
        bb = bias
        if isinstance(bias, tuple):
            rd += bias[1]
            bb = bias[0]
        if isinstance(scale, tuple):
            rd += scale[1]
            scale = scale[0]
        if acc is not None:
            wr += acc[1]
            op("s", [lambda: g.scalar.activation(out[0], in_[0], func, bias=bb, scale=scale, accum_out=acc[0])], rd, wr)
        else:
            op("s", [lambda: g.scalar.activation(out[0], in_[0], func, bias=bb, scale=scale)], rd, wr)

    def tt(out, a, b, o):
        op("v", [lambda: g.vector.tensor_tensor(out[0], a[0], b[0], o)], a[1] + b[1], out[1])

    def ts(out, a, s1, o1, s2=None, o2=None):
        rd = list(a[1])
        v = []
        for s in (s1, s2):
            if isinstance(s, tuple):
                rd += s[1]
                v.append(s[0])
            else:
                v.append(s)
        if o2 is None:
            op("v", [lambda: g.vector.tensor_scalar(out[0], a[0], v[0], None, o1)], rd, out[1])
        else:
            op("v", [lambda: g.vector.tensor_scalar(out[0], a[0], v[0], v[1], o1, o2)], rd, out[1])

    def scan(out, d0, d1, init, o1, o2):
        rd = d0[1] + d1[1]
        ii = init
        if isinstance(init, tuple):
            rd = rd + init[1]
            ii = init[0]
        op("v", [lambda: g.vector.tensor_tensor_scan(out[0], d0[0], d1[0], ii, o1, o2)], rd, out[1])

    def fill(reg, val):
        op("v", [lambda: g.vector.memset(reg[0], val)], [], reg[1])

    def mm(out, pairs, start=True, stop=True):
        rd, fns = [], []
        for k, (l, r) in enumerate(pairs):
            rd += l[1] + r[1]
            fns.append(lambda l=l, r=r, k=k: g.tensor.matmul(out[0], l[0], r[0], start and k == 0, stop and k == len(pairs) - 1))
        op("p", fns, rd, out[1], not start)

    def iota(reg, pattern, base, cm, flag=True):
        if flag:
            op("g", [lambda: g.iota(reg[0], pattern, base, cm, allow_small_or_imprecise_dtypes=True)], [], reg[1])
        else:
            op("g", [lambda: g.iota(reg[0], pattern, base, cm)], [], reg[1])

    def asel(out, in_, pattern, cmp, base, cm):
        op("g", [lambda: g.affine_select(out[0], in_[0], pattern, cmp, 0.0, base, cm)], in_[1], out[1])

    def M(name, j=0):
        return R(name, 128 * j, 128 * j + 128)

    def C(j):
        return R("cf", j, j + 1)

    def shift(n, w):
        k = abs(n) // 16
        return (R("cm", 0 if n < 0 else 128, 128 if n < 0 else 256, 1, k), R("ones", 0, w, 1, k))

    dma("y", T.wtc[:], T.wt[:], [], [("wtc", 0, 1)])
    dma("s", T.X[:, 2048:S], T.x0[:, 2048:S], [], [("X", 2048, S)])
    dma("y", T.kq[:], T.kd[:], [], [("kq", 0, 256)])
    dma("s", T.thc[:], T.th[:], [], [("thc", 0, 1)])
    dma("s", T.X[:, 0:1024], T.x0[:, 0:1024], [], [("X", 0, 1024)])
    dma("y", T.X[:, 1024:2048], T.x0[:, 1024:2048], [], [("X", 1024, 2048)])
    dma("y", T.tac[:], T.tau[:], [], [("tac", 0, 1)])

    iota(R("ci", 0, 1), [[0, 1]], 0, 1, False)
    iota(R("pj", 0, 9), [[-1, 9]], 0, 1)
    iota(M("ib", 0), [[1, 8], [8, 16]], 0, 0)
    iota(R("pj", 16, 32), [[8, 16]], 0, 0)
    iota(M("ib", 1), [[0, 8], [8, 16]], 0, 0)
    iota(M("ib", 2), [[1, 8], [0, 16]], 0, 0)
    iota(R("k613", 0, 12), [[613 * 16, 12]], 0, 0)
    fill(R("ones", 0, 512), 1.0)
    ts(R("ci", 2, 3), R("ci", 0, 1), 4, Op.arith_shift_right)
    ts(R("ci", 1, 2), R("ci", 0, 1), 15, Op.bitwise_and)
    scan(R("io16", 0, 512), R("ones", 0, 512), R("ones", 0, 512), -1.0, Op.mult, Op.add)
    cp("v", C(1), R("ci", 2, 3))
    for j, v in enumerate((-16.0, 16.0, -1.0 / 128)):
        act(M("cm", j), M("ones"), Fn.Copy, scale=v)
    act(R("nxb", NP, 208), R("ones", 0, 16), Fn.Copy, scale=0.0)
    io, row = R("io16", 0, 128), R("pj", 0, 1)
    ts(M("idp"), io, row, Op.is_equal)
    ts(R("pj", 16, 32), R("pj", 16, 32), C(1), Op.add)
    ts(C(3), R("ci", 1, 2), 8, Op.is_lt)
    ts(C(4), R("ci", 1, 2), 8, Op.is_ge)
    ts(C(5), row, 8.0, Op.add)
    for nm, v in (("idn", -1.0), ("idh", 0.5), ("idk", -K)):
        act(M(nm), M("idp"), Fn.Copy, scale=v)
    act(M("pm", 0), M("idp"), Fn.Copy, scale=C(3))
    act(M("pm", 3), M("idp"), Fn.Copy, scale=C(4))
    for b in range(4):
        mm(Q(b, 0, 512), [(M("idp"), R("io16", 0, 512)), shift(512 * b - MID, 512)])
    for j in range(16):
        ts(M("om", j), M("ib", 0), R("pj", 16 + j, 17 + j), Op.is_equal)
    for j in range(8):
        ts(M("ksel", j), M("ib", 1), R("pj", j, j + 1), Op.is_equal)
    cp("v", R("thf", 0, 1), R("thc", 0, 1))
    cp("v", R("wtf", 0, 1), R("wtc", 0, 1))
    iota(R("m8n", 0, 512), [[0, 64], [-20480, 8]], 16384, 0)
    iota(R("m8x", 0, 512), [[0, 64], [20480, 8]], -16384, 0)
    iota(R("m16x", 0, 1024), [[0, 64], [256, 16]], 0, 0)
    iota(R("m16n", 0, 1024), [[0, 64], [-256, 16]], 256, 0)
    iota(R("iom", 0, RO * FO * CAP), [[G, RO], [1, FO * CAP]], S + NP - MID, 0)
    iota(R("An", 0, RO * G), [[1, RO * G]], S, 0)

    def prepu(t):
        src = ("X", S - G) if t == 0 else ("nxb", 0)
        mm(R("pU", 0, 12), [(M("wm", p), R(src[0], src[1] + p, src[1] + NP, 16)) for p in range(16)])

    def prep():
        tt(R("ui", 0, 12), R("pU", 0, 12), R("k613", 0, 12), Op.add)
        yield
        ts(R("um", 0, 12), R("ui", 0, 12), U - 1, Op.bitwise_and)
        yield
        cp("v", R("uo", 0, 12), R("um", 0, 12))
        yield
        cp("v", R("ke", 0, NP), I("kdt", 0, U, "uo", 0, 12))
        ev, od = R("ke", 0, NP, 2), R("ke", 1, NP, 2)
        mm(R("pU", 0, 96), [(M("pm", 0), ev), (M("pm", 1), od)])
        mm(R("pU", 96, 192), [(M("pm", 2), ev), (M("pm", 3), od)])
        yield

    def prep2(t):
        sc, off = (10 + t) / 16.0, 128.0 * (10 + t) - 15.0 / 32
        ts(R("t1", 0, 96), R("pU", 0, 96), sc, Op.mult, off, Op.add)
        ts(R("t2", 0, 96), R("pU", 96, 192), sc, Op.mult, off, Op.add)

    rot = ["pD", "pX", "pC"]
    nrot = [0]

    def bank():
        nrot[0] += 1
        return rot[nrot[0] % 3]

    def spread(b, q):
        pn = bank()
        for h in range(2):
            mm(R(pn, 256 * h, 256 * h + 256), [(M("ksel", 2 * b + h), R("k16", 0, 256))])
        cp(q, R("kdt", 512 * b, 512 * b + 512), R(pn, 0, 512))

    def s8(b):
        ts(R("s8", 512 * b, 512 * b + 512), R("X", 512 * b, 512 * b + 512), R("thf", 0, 1), Op.is_lt, K, Op.mult)

    def code(win, b):
        pn = bank()
        mm(R(pn, 0, 512), [(M("idp"), R("io16", 0, 512)), (M("idp" if win == "Wl" else "idn"), R("s8", 512 * b, 512 * b + 512))])
        act(R(win, 512 * b, 512 * b + 512), R(pn, 0, 512), Fn.Identity, bias=float(512 * b - MID))

    def codev(b):
        tt(R("Wl", 512 * b, 512 * b + 512), Q(b, 0, 512), R("s8", 512 * b, 512 * b + 512), Op.add)

    s8(4)
    code("Wl", 4)
    code("Wh", 4)
    ts(C(2), R("ci", 1, 2), 613.0, Op.mult)
    ts(R("k16", 0, 256), R("kq", 0, 256), -2048.0, Op.add)
    ts(R("wm", 0, 2048), R("om", 0, 2048), R("wtf", 0, 1), Op.mult)
    spread(0, "s")
    s8(0)
    s8(1)
    spread(1, "v")
    spread(2, "s")
    prepu(0)
    spread(3, "s")
    ts(R("k613", 0, 12), R("k613", 0, 12), C(2), Op.add)
    code("Wh", 0)
    code("Wh", 1)
    pr = prep()
    next(pr)
    ts(M("pm", 1), io, C(5), Op.is_equal, C(3), Op.mult)
    next(pr)
    ts(M("pm", 2), io, R("pj", 8, 9), Op.is_equal, C(4), Op.mult)
    next(pr)
    s8(2)
    s8(3)
    next(pr)
    code("Wh", 2)
    code("Wh", 3)
    codev(0)
    codev(1)
    prep2(0)
    codev(2)
    codev(3)

    def later():
        ts(M("blk"), M("ib", 2), C(1), Op.is_equal)
        yield
        ts(C(7), R("ci", 1, 2), 0.5, Op.add)
        yield
        ts(C(8), R("ci", 1, 2), 16.5, Op.add)
        yield
        cp("v", R("thr", 0, 1), R("tac", 0, 1))
        while True:
            yield

    late = later()
    nloc = 0

    for t in range(RO):
        B = S + t * G

        def step(name, c, c1, B=B):
            i0, i1 = UNIT * c, UNIT * (c1 + 1)
            n = i1 - i0
            w8, w16, li = (8 * i0, 8 * i1), (16 * i0, 16 * i1), (i0 // 2, i1 // 2)
            end8, end16 = (8 * i0 + 7, 8 * i1, 8), (16 * i0 + 15, 16 * i1, 16)
            nb = c % 4
            blocks = [(nb + k, 16 * i0 + a, 16 * i0 + min(a + 512, 16 * n)) for k, a in enumerate(range(0, 16 * n, 512))]
            pd = R("pD" if i1 < NP else "pX", i0, i1)
            q = "s" if name.islower() else "v"
            if name in "lL":
                cp(q, R("L1", *w8), I("Wl", 0, B, "t1", *li))
            elif name in "hH":
                cp(q, R("H1", *w8), I("Wh", 0, B, "t1", *li))
            elif name == "c":
                act(R("c0", i0, i1), R("L1", 8 * i0, 8 * i1, 8), Fn.Identity, bias=-K)
            elif name == "C":
                ts(R("c0", i0, i1), R("L1", 8 * i0, 8 * i1, 8), -K, Op.add)
            elif name == "A":
                tt(R("al", *w8), I("Wl", 0, B, "t2", *li), R("L1", *w8), Op.min)
            elif name == "B":
                tt(R("ah", *w8), I("Wh", 0, B, "t2", *li), R("H1", *w8), Op.max)
            elif name == "s":
                scan(R("sl", *w8), R("m8n", 0, 8 * n), R("al", *w8), 0.0, Op.max, Op.min)
            elif name == "t":
                scan(R("sh", *w8), R("m8x", 0, 8 * n), R("ah", *w8), 0.0, Op.min, Op.max)
            elif name == "p":
                tt(R("yy", i0, i1), R("sh", *end8), R("c0", i0, i1), Op.max)
            elif name == "q":
                tt(R("lo", i0, i1), R("sl", *end8), R("yy", i0, i1), Op.min)
            elif name == "r":
                ts(R("ol", i0, i1), R("lo", i0, i1), float(MID), Op.add)
            elif name == "u":
                tt(R("hi", i0, i1), R("sh", *end8), R("lo", i0, i1), Op.max)
            elif name == "v":
                ts(R("oh", i0, i1), R("hi", i0, i1), float(MID), Op.add)
            elif name in "xX":
                cp(q, R("XL", *w16), I("X", 0, B, "ol", i0, i1))
            elif name in "yY":
                cp(q, R("XH", *w16), I("X", 0, B, "oh", i0, i1))
            elif name in "ed":
                for pn, a, e in blocks:
                    mm(Q(pn, 0, e - a), [(M("idp" if name == "e" else "idn"), R("XL" if name == "e" else "XH", a, e))], name == "e", name == "d")
            elif name == "b":
                act(R("ad", *w16), Q(nb, 0, 16 * n), Fn.Abs)
            elif name == "D":
                mm(pd, [(M("om", p), R("ad", 16 * i0 + p, 16 * i1, 16)) for p in range(16)])
            elif name == "m":
                scan(R("mxs", *w16), R("m16x", 0, 16 * n), R("XL", *w16), 0.0, Op.min, Op.max)
            elif name == "n":
                scan(R("mns", *w16), R("m16n", 0, 16 * n), R("XH", *w16), 0.0, Op.max, Op.min)
            elif name == "a":
                mm(R("pU", 256 + i0, 256 + i1), [(M("idh"), R("mxs", *end16)), (M("idh"), R("mns", *end16)),
                                                 (R("cm", 256, 384, 1, 32), R("ones", 0, n, 1, 32))])
            elif name == "w":
                ts(R("nxb", i0, i1), R("pU", 256 + i0, 256 + i1), RND, Op.add, -RND, Op.add)
            elif name == "f":
                ts(R("near", i0, i1), pd, R("thr", 0, 1), Op.is_le)
            elif name == "k":
                mm(R("pC", i0, i1), [(M("blk"), R("near", i0, i1))])
            elif name == "g":
                ts(R("flg", i0, i1), R("pC", i0, i1), 15.5, Op.is_lt)
            elif name == "j":
                scan(R("cum", i0, i1), R("ones", i0, i1), R("flg", i0, i1), 0.0 if c == 0 else R("cum", i0 - 1, i0), Op.mult, Op.add)
            elif name == "z":
                for h in range(2):
                    k = h + (2 if c else 0)
                    act(R("sg", h * NP + i0, h * NP + i1), R("cum", i0, i1), Fn.Sign, bias=C(7 + h), scale=-1.0, acc=R("cnt2", k, k + 1))
            elif name == "Z":
                ts(R("cnt2", 4, 6), R("cnt2", 0, 2), float(NP), Op.add)
            if name in "pqu":
                next(late)

        for st in ORDER.split():
            step(st[0], int(st[1]), int(st[-1]))

        more = t + 1 < RO
        if more:
            prepu(t + 1)
        mm(Q(0, 0, NP), [(M("idp"), R("io16", 0, NP)), shift(B - MID, NP), (M("idk"), R("near", 0, NP))])
        if more:
            ts(R("e8", 0, NP), R("nxb", 0, NP), R("thf", 0, 1), Op.is_lt, K, Op.mult)
            pr = prep()
            next(pr)
        for h in range(2):
            ts(R("mo", h, h + 1), R("cnt2", 2 + h, 3 + h), R("cnt2", 4 + h, 5 + h), Op.add, 0.5, Op.mult)
        if more:
            next(pr)
        cp("v", R("mailb", t * CAP, (t + 1) * CAP), I("nxb", 0, 208, "mo", 0, 2))
        direct, via = plan[rank, t]
        ml = T.mailb[:, t * CAP:(t + 1) * CAP]
        dowait("g", need("g", [("mailb", t * CAP, (t + 1) * CAP)], []))
        tr = []
        if via:
            ids = []
            for rc in relay[rank][:len(via)]:
                rid, pid = topo.addr(rc, core)
                ids.append(DstId(rid=rid, pnc=pid))
            m, k = emask(topo, core, relay[rank][0], True, not direct)
            nloc += k
            tr.append(RemoteDMATransfer(dst_ids=ids, dma_engine_mask=m, remote_sem=T.sem["rl%d" % t], srcs=[ml],
                                        dsts=[T.rbuf[:, t * CAP:(t + 1) * CAP] for rc in ids]))
        if direct:
            ids, outs = [], []
            for f, d in direct:
                rid, pid = topo.addr(d, core)
                ids.append(DstId(rid=rid, pnc=pid))
                a, b = land(t, f)
                outs.append(T.X[:, a:b])
            m, k = emask(topo, core, direct[0][1], False)
            nloc += k
            tr.append(RemoteDMATransfer(dst_ids=ids, dma_engine_mask=m, remote_sem=T.sem["ar%d" % t], srcs=[ml], dsts=outs))
        g.remote_dma_fused(tr, local_sem=T.sem.loc)

        j0 = t * G
        cp("s", R("X", B, B + NP), R("nxb", 0, NP))
        if more:
            next(pr)
        tt(R("A16", 0, NP), Q(0, 0, NP), R("lo", 0, NP), Op.max)
        if more:
            next(pr)
            mm(R("pC", 256, 257), [(M("ones"), R("cum", NP - 1, NP))])
            for win, idm, pn in (("Wl", "idp", 1), ("Wh", "idn", 2)):
                mm(Q(pn, 0, NP), [(M("idp"), R("A16", 0, NP)), (M(idm), R("e8", 0, NP))])
                cp("s", R(win, B, B + NP), Q(pn, 0, NP))
            cp("v", R("cci", 0, 1), R("pC", 256, 257))
            prep2(t + 1)
            ts(R("cci", 1, 2), R("cci", 0, 1), 4, Op.arith_shift_right, 15, Op.bitwise_and)
        ts(R("An", j0, j0 + NP), R("A16", 0, NP), float(MID), Op.add)
        if more:
            tt(R("thr", 0, 1), R("cci", 1, 2), R("tac", 0, 1), Op.add)
        dma("y", T.yx[:, j0:j0 + NP], T.X[:, B:B + NP], [("X", B, B + NP)], [])
        dma("y", T.ya[:, j0:j0 + G], T.An[:, j0:j0 + G], [("An", j0, j0 + G)], [])

        key = "ar%d" % t
        narr = 0
        for f in range(FO):
            s = T.cores[(rank - 1 - ((FO * t + f) % (len(T.cores) - 1))) % len(T.cores)]
            if not topo.may_write(s, core):
                s = relay[T.rank_of(s)][0]
            narr += emask(topo, s, core, False)[1]
        semof[key] = T.sem[key]
        clock[key, narr] = {}
        note(key, narr, [], [("X", B + NP, B + G)])
        if more:
            names = R("iom", t * FO * CAP, (t + 1) * FO * CAP)
            ts(R("e8", NP, G), R("X", B + NP, B + G), R("thf", 0, 1), Op.is_lt, K, Op.mult)
            tt(R("Wl", B + NP, B + G), names, R("e8", NP, G), Op.add)
            tt(R("Wh", B + NP, B + G), names, R("e8", NP, G), Op.subtract)
        dma("y", T.yx[:, j0 + NP:j0 + G], T.X[:, B + NP:B + G], [("X", B + NP, B + G)], [])

    g.wait_ge(T.sem.loc, nloc)
    for q in ("v", "s", "p", "g"):
        g.wait_ge(semof[q], count[q])
    for k in range(ndma[0]):
        g.wait_ge(T.sem["d%d" % k], 16)
